import numpy as np
import ml_dtypes


def mxq(x, axis, fmt="e4m3"):
    dtype, down = {"e4m3": (ml_dtypes.float8_e4m3fn, 7), "e5m2": (ml_dtypes.float8_e5m2, 14)}[fmt]
    v = np.moveaxis(np.asarray(x, np.float32).astype(ml_dtypes.bfloat16).astype(np.float64), axis, -1)
    blocks = v.reshape(v.shape[:-1] + (-1, 32))
    amax = np.abs(blocks).max(-1, keepdims=True)
    byte = np.maximum(np.where(amax > 0, np.frexp(amax)[1] - 1 + 127, 0) - down, 1)
    scale = np.exp2(byte - 127.0)
    codes = (blocks / scale).astype(np.float32).astype(dtype).astype(np.float64)
    return np.moveaxis((codes * scale).reshape(v.shape), -1, axis)


WIDE = False


def mx_kscale(k):
    if not WIDE:
        return np.ones(k)
    levels = np.array([10, -10, 5, -5, 0])
    if k % 512:
        return np.exp2(np.random.permutation(np.resize(levels, k // 32))).repeat(32)
    a = np.empty((k // 512, 16))
    for p in range(k // 512):
        a[p, :8] = np.random.permutation(np.resize(levels, 8))
        for g in range(8):
            far = levels[np.abs(levels - a[p, g]) >= 10]
            a[p, g + 8] = far[np.random.randint(len(far))]
    return np.exp2(a.ravel()).repeat(32)


def f64(x):
    return np.asarray(x).astype(np.float64)


def striped(idx):
    return np.tile(idx.reshape(-1, 16).T, (8, 1)).astype(np.uint16)


def unstriped(offs):
    return offs[:16].T.reshape(-1).astype(np.int64)


K, T, S, V, N = 1024, 2048, 512, 256, 128


def setup_inputs():
    n = np.random.standard_normal
    s = mx_kscale(K)[:, None]
    return {
        "xT": (n((K, T)) * s).astype(np.float32),
        "w1": (n((K, N)) / np.sqrt(K) / s).astype(np.float32),
        "offs": striped(np.random.permutation(T)[:S]),
        "pos1": striped(np.random.permutation(S)[:V]),
        "pos2": striped(np.random.permutation(S)[:V]),
        "pos3": striped(np.random.permutation(S)[:V]),
    }


def reference(xT, w1, offs, pos1, pos2, pos3):
    xq = mxq(f64(xT)[:, unstriped(offs)], 0, "e4m3")
    y = mxq(f64(w1), 0, "e4m3").T @ xq
    n0 = y[:, unstriped(pos1)]
    n1 = y[:, unstriped(pos2)]
    n2 = y[:, unstriped(pos3)]
    return np.maximum(np.minimum(n0, n1), np.minimum(np.maximum(n0, n1), n2))

@@ -1,0 +1,132 @@
+from contextlib import ExitStack
+
+import concourse.mybir as mybir
+
+K, T, S, V, N = 1024, 2048, 512, 256, 128
+FLOPS = 2 * K * S * N
+
+F32 = mybir.dt.float32
+BF16 = mybir.dt.bfloat16
+U32 = mybir.dt.uint32
+U16 = mybir.dt.uint16
+U8 = mybir.dt.uint8
+FP8X4 = mybir.dt.float8_e4m3fn_x4
+MAX = mybir.AluOpType.max
+MIN = mybir.AluOpType.min
+
+P = 128
+PACK = 4
+K_PASS = P * PACK
+PASSES = K // K_PASS
+LANES = 16
+HALF = S // 2
+QUARTER = S // 4
+V_HALF = V // 2
+
+
+def tile_picked_median_none_e_kernel(tc, xT, w1, offs, pos1, pos2, pos3, out):
+    nc = tc.nc
+    with ExitStack() as ctx:
+        keep = ctx.enter_context(tc.tile_pool(name="keep", bufs=1))
+        psum = ctx.enter_context(tc.psum_pool(name="psum", bufs=1))
+
+        x_rows = xT.rearrange("(z p j) t -> z j p t", p=P, j=PACK)
+        w_rows = w1.rearrange("(z p j) n -> z p j n", p=P, j=PACK)
+
+        picked = keep.tile([P, S // LANES], U16, name="picked")
+        planes = []
+        for z in range(PASSES):
+            for j in range(PACK):
+                plane = keep.tile([P, T], F32, name="plane%d_%d" % (z, j))
+                nc.sync.dma_start(out=plane[:], in_=x_rows[z, j])
+                planes.append(plane)
+                if z == 0 and j == 0:
+                    nc.sync.dma_start(out=picked[:], in_=offs)
+        w_raw = []
+        for z in range(PASSES):
+            raw = keep.tile([P, PACK, N], F32, name="w_raw%d" % z)
+            nc.sync.dma_start(out=raw[:], in_=w_rows[z])
+            w_raw.append(raw)
+        places = []
+        for d, pos in enumerate((pos1, pos2, pos3)):
+            place = keep.tile([P, V // LANES], U16, name="place%d" % d)
+            nc.sync.dma_start(out=place[:], in_=pos)
+            places.append(place)
+
+        x_bf = [keep.tile([P, S, PACK], BF16, name="x_bf%d" % z, align_bytes=64) for z in range(PASSES)]
+
+        def gather(z, j, lo, hi):
+            window = planes[z * PACK + j]
+            nc.vector.tensor_copy(out=x_bf[z][:, lo:hi, j], in_=window[:].indirect(picked[:, lo // LANES : hi // LANES]))
+
+        def quantize(src, width, name, tag):
+            codes = keep.tile([P, width], U32, name=name + "_codes", tag=tag, align_bytes=64)
+            scales = keep.tile([P, width], U8, name=name + "_scales", align_bytes=64)
+            nc.vector.quantize_mx(out=codes[:].bitcast(FP8X4), scales=scales[:], in_=src.rearrange("p c j -> p (c j)"))
+            return codes, scales
+
+        def weave_w(z):
+            w_bf = keep.tile([P, N, PACK], BF16, name="w_bf%d" % z, tag="shared%d" % z, align_bytes=64)
+            nc.scalar.copy(out=w_bf[:], in_=w_raw[z][:].rearrange("p j n -> p n j"))
+            return quantize(w_bf[:], N, "w%d" % z, "w%d_codes" % z)
+
+        for j in range(PACK):
+            gather(0, j, 0, S)
+        x0_codes, x0_scales = quantize(x_bf[0][:], S, "x0", "x0_codes")
+        for j in range(PACK - 1):
+            gather(1, j, 0, S)
+        for h in range(2):
+            gather(1, PACK - 1, h * HALF, (h + 1) * HALF)
+
+        pieces = ((0, HALF), (HALF, HALF + QUARTER), (HALF + QUARTER, S))
+        acc = [psum.tile([P, c1 - c0], F32, name="acc%d" % i) for i, (c0, c1) in enumerate(pieces)]
+        w0_codes, w0_scales = weave_w(0)
+        for i, (c0, c1) in enumerate(pieces):
+            nc.tensor.matmul_mx(
+                out=acc[i][:],
+                lhsT=w0_codes[:].bitcast(FP8X4),
+                lhsT_scale=w0_scales[:],
+                rhs=x0_codes[:, c0:c1].bitcast(FP8X4),
+                rhs_scale=x0_scales[:, c0:c1],
+                start=True,
+                stop=False,
+            )
+        x1 = [quantize(x_bf[1][:, 0:HALF, :], HALF, "x1_0", "shared0")]
+        w1_codes, w1_scales = weave_w(1)
+        x1.append(quantize(x_bf[1][:, HALF : HALF + QUARTER, :], QUARTER, "x1_1", "shared1"))
+        x1.append(quantize(x_bf[1][:, HALF + QUARTER : S, :], QUARTER, "x1_2", "x1_2_codes"))
+
+        y = keep.tile([P, S], F32, name="y")
+        for i, (c0, c1) in enumerate(pieces):
+            nc.tensor.matmul_mx(
+                out=acc[i][:],
+                lhsT=w1_codes[:].bitcast(FP8X4),
+                lhsT_scale=w1_scales[:],
+                rhs=x1[i][0][:].bitcast(FP8X4),
+                rhs_scale=x1[i][1][:],
+                start=False,
+                stop=True,
+            )
+            if i == 1:
+                nc.vector.tensor_copy(out=y[:, c0:c1], in_=acc[i][:])
+            else:
+                nc.scalar.copy(out=y[:, c0:c1], in_=acc[i][:])
+
+        near = []
+        for d in range(3):
+            got = keep.tile([P, V], F32, name="near%d" % d)
+            nc.vector.tensor_copy(out=got[:], in_=y[:].indirect(places[d][:]))
+            near.append(got)
+        hi = keep.tile([P, V], F32, name="hi")
+        lo = keep.tile([P, V], F32, name="lo")
+        nc.vector.tensor_tensor(out=hi[:], in0=near[0][:], in1=near[1][:], op=MAX)
+        nc.vector.tensor_tensor(out=lo[:], in0=near[0][:], in1=near[1][:], op=MIN)
+        capped = keep.tile([P, V], F32, name="capped")
+        for h in range(2):
+            cols = slice(h * V_HALF, (h + 1) * V_HALF)
+            nc.vector.tensor_tensor(out=capped[:, cols], in0=hi[:, cols], in1=near[2][:, cols], op=MIN)
+        for h in range(2):
+            cols = slice(h * V_HALF, (h + 1) * V_HALF)
+            med = keep.tile([P, V_HALF], F32, name="med%d" % h)
+            nc.vector.tensor_tensor(out=med[:], in0=lo[:, cols], in1=capped[:, cols], op=MAX)
+            nc.sync.dma_start(out=out[:, cols], in_=med[:])

@@ -30,18 +30,17 @@ def tile_picked_median_none_e_kernel(tc, xT, w1, offs, pos1, pos2, pos3, out):
         keep = ctx.enter_context(tc.tile_pool(name="keep", bufs=1))
         psum = ctx.enter_context(tc.psum_pool(name="psum", bufs=1))
 
-        x_rows = xT.rearrange("(z p j) t -> z j p t", p=P, j=PACK)
         w_rows = w1.rearrange("(z p j) n -> z p j n", p=P, j=PACK)
 
         picked = keep.tile([P, S // LANES], U16, name="picked")
+        x_pairs = xT.rearrange("(z p j) t -> z p j t", p=P, j=PACK)
         planes = []
-        for z in range(PASSES):
-            for j in range(PACK):
-                plane = keep.tile([P, T], F32, name="plane%d_%d" % (z, j))
-                nc.sync.dma_start(out=plane[:], in_=x_rows[z, j])
-                planes.append(plane)
-                if z == 0 and j == 0:
-                    nc.sync.dma_start(out=picked[:], in_=offs)
+        for z, j0, j1 in ((0, 0, 2), (0, 2, 4), (1, 0, 2), (1, 2, 3), (1, 3, 4)):
+            rows = keep.tile([P, j1 - j0, T], F32, name="rows%d_%d" % (z, j0))
+            nc.sync.dma_start(out=rows[:], in_=x_pairs[z, :, j0:j1, :])
+            planes.extend(rows[:, j, :] for j in range(j1 - j0))
+            if z == 0 and j0 == 0:
+                nc.sync.dma_start(out=picked[:], in_=offs)
         w_raw = []
         for z in range(PASSES):
             raw = keep.tile([P, PACK, N], F32, name="w_raw%d" % z)
@@ -57,7 +56,7 @@ def tile_picked_median_none_e_kernel(tc, xT, w1, offs, pos1, pos2, pos3, out):
 
         def gather(z, j, lo, hi):
             window = planes[z * PACK + j]
-            nc.vector.tensor_copy(out=x_bf[z][:, lo:hi, j], in_=window[:].indirect(picked[:, lo // LANES : hi // LANES]))
+            nc.vector.tensor_copy(out=x_bf[z][:, lo:hi, j], in_=window.indirect(picked[:, lo // LANES : hi // LANES]))
 
         def quantize(src, width, name, tag):
             codes = keep.tile([P, width], U32, name=name + "_codes", tag=tag, align_bytes=64)
@@ -73,8 +72,11 @@ def tile_picked_median_none_e_kernel(tc, xT, w1, offs, pos1, pos2, pos3, out):
         for j in range(PACK):
             gather(0, j, 0, S)
         x0_codes, x0_scales = quantize(x_bf[0][:], S, "x0", "x0_codes")
-        for j in range(PACK - 1):
-            gather(1, j, 0, S)
+        plain = keep.tile([P, 2, S], F32, name="plain")
+        for j in range(2):
+            nc.vector.tensor_copy(out=plain[:, j, :], in_=planes[PACK + j].indirect(picked[:]))
+        nc.scalar.copy(out=x_bf[1][:, :, 0:2], in_=plain[:].rearrange("p j c -> p c j"))
+        gather(1, 2, 0, S)
         for h in range(2):
             gather(1, PACK - 1, h * HALF, (h + 1) * HALF)
 
@@ -91,10 +93,19 @@ def tile_picked_median_none_e_kernel(tc, xT, w1, offs, pos1, pos2, pos3, out):
                 start=True,
                 stop=False,
             )
-        x1 = [quantize(x_bf[1][:, 0:HALF, :], HALF, "x1_0", "shared0")]
+        early_codes, early_scales = quantize(x_bf[1][:, 0:HALF, :], HALF, "x1_0", "shared0")
+        x1 = [(early_codes[:], early_scales[:])]
         w1_codes, w1_scales = weave_w(1)
-        x1.append(quantize(x_bf[1][:, HALF : HALF + QUARTER, :], QUARTER, "x1_1", "shared1"))
-        x1.append(quantize(x_bf[1][:, HALF + QUARTER : S, :], QUARTER, "x1_2", "x1_2_codes"))
+        late_codes = keep.tile([P, HALF], U32, name="late_codes", tag="shared1", align_bytes=64)
+        late_scales = keep.tile([P, HALF], U8, name="late_scales", align_bytes=64)
+        for c0, c1 in pieces[1:]:
+            cols = slice(c0 - HALF, c1 - HALF)
+            nc.vector.quantize_mx(
+                out=late_codes[:, cols].bitcast(FP8X4),
+                scales=late_scales[:, cols],
+                in_=x_bf[1][:, c0:c1, :].rearrange("p c j -> p (c j)"),
+            )
+            x1.append((late_codes[:, cols], late_scales[:, cols]))
 
         y = keep.tile([P, S], F32, name="y")
         for i, (c0, c1) in enumerate(pieces):
@@ -102,8 +113,8 @@ def tile_picked_median_none_e_kernel(tc, xT, w1, offs, pos1, pos2, pos3, out):
                 out=acc[i][:],
                 lhsT=w1_codes[:].bitcast(FP8X4),
                 lhsT_scale=w1_scales[:],
-                rhs=x1[i][0][:].bitcast(FP8X4),
-                rhs_scale=x1[i][1][:],
+                rhs=x1[i][0].bitcast(FP8X4),
+                rhs_scale=x1[i][1],
                 start=False,
                 stop=True,
             )

@@ -66,7 +66,10 @@ def tile_picked_median_none_e_kernel(tc, xT, w1, offs, pos1, pos2, pos3, out):
 
         def weave_w(z):
             w_bf = keep.tile([P, N, PACK], BF16, name="w_bf%d" % z, tag="shared%d" % z, align_bytes=64)
-            nc.scalar.copy(out=w_bf[:], in_=w_raw[z][:].rearrange("p j n -> p n j"))
+            nc.scalar.copy(
+                out=w_bf[:].rearrange("p (c i) j -> p c j i", i=PACK),
+                in_=w_raw[z][:].rearrange("p j (c i) -> p c j i", i=PACK),
+            )
             return quantize(w_bf[:], N, "w%d" % z, "w%d_codes" % z)
 
         for j in range(PACK):

@@ -35,7 +35,7 @@ def tile_picked_median_none_e_kernel(tc, xT, w1, offs, pos1, pos2, pos3, out):
         picked = keep.tile([P, S // LANES], U16, name="picked")
         x_pairs = xT.rearrange("(z p j) t -> z p j t", p=P, j=PACK)
         planes = []
-        for z, j0, j1 in ((0, 0, 2), (0, 2, 4), (1, 0, 2), (1, 2, 3), (1, 3, 4)):
+        for z, j0, j1 in ((0, 0, 2), (0, 2, 4), (1, 0, 1), (1, 1, 2), (1, 2, 3), (1, 3, 4)):
             rows = keep.tile([P, j1 - j0, T], F32, name="rows%d_%d" % (z, j0))
             nc.sync.dma_start(out=rows[:], in_=x_pairs[z, :, j0:j1, :])
             planes.extend(rows[:, j, :] for j in range(j1 - j0))
@@ -72,8 +72,13 @@ def tile_picked_median_none_e_kernel(tc, xT, w1, offs, pos1, pos2, pos3, out):
             )
             return quantize(w_bf[:], N, "w%d" % z, "w%d_codes" % z)
 
+        plain0 = keep.tile([P, PACK, S], F32, name="plain0")
         for j in range(PACK):
-            gather(0, j, 0, S)
+            nc.vector.tensor_copy(out=plain0[:, j, :], in_=planes[j].indirect(picked[:]))
+        nc.scalar.copy(
+            out=x_bf[0][:].rearrange("p (c i) j -> p c j i", i=PACK),
+            in_=plain0[:].rearrange("p j (c i) -> p c j i", i=PACK),
+        )
         x0_codes, x0_scales = quantize(x_bf[0][:], S, "x0", "x0_codes")
         plain = keep.tile([P, 2, S], F32, name="plain")
         for j in range(2):

@@ -33,17 +33,19 @@ def tile_picked_median_none_e_kernel(tc, xT, w1, offs, pos1, pos2, pos3, out):
         w_rows = w1.rearrange("(z p j) n -> z p j n", p=P, j=PACK)
 
         picked = keep.tile([P, S // LANES], U16, name="picked")
-        x_pairs = xT.rearrange("(z p j) t -> z p j t", p=P, j=PACK)
+        x_pass = xT.rearrange("(z p j) t -> z p j t", p=P, j=PACK)
+        gap = K_PASS - (PACK - 1)
+        across = xT[PACK - 1 : PACK - 1 + 2 * gap, :].rearrange("(r q) t -> q r t", r=2)[0:gap:PACK]
         planes = []
-        for z, j0, j1 in ((0, 0, 2), (0, 2, 4), (1, 0, 1), (1, 1, 2), (1, 2, 3), (1, 3, 4)):
-            rows = keep.tile([P, j1 - j0, T], F32, name="rows%d_%d" % (z, j0))
-            nc.sync.dma_start(out=rows[:], in_=x_pairs[z, :, j0:j1, :])
-            planes.extend(rows[:, j, :] for j in range(j1 - j0))
-            if z == 0 and j0 == 0:
+        for i, src in enumerate((x_pass[0, :, 0:3, :], across, x_pass[1, :, 1:2, :], x_pass[1, :, 2:3, :], x_pass[1, :, 3:4, :])):
+            rows = keep.tile([P, src.shape[1], T], F32, name="rows%d" % i)
+            nc.sync.dma_start(out=rows[:], in_=src)
+            planes.extend(rows[:, j, :] for j in range(src.shape[1]))
+            if i == 0:
                 nc.sync.dma_start(out=picked[:], in_=offs)
         w_raw = []
         for z in range(PASSES):
-            raw = keep.tile([P, PACK, N], F32, name="w_raw%d" % z)
+            raw = keep.tile([P, PACK, N], F32, name="w_raw%d" % z, tag="shared%d" % z, align_bytes=64)
             nc.sync.dma_start(out=raw[:], in_=w_rows[z])
             w_raw.append(raw)
         places = []
@@ -65,7 +67,7 @@ def tile_picked_median_none_e_kernel(tc, xT, w1, offs, pos1, pos2, pos3, out):
             return codes, scales
 
         def weave_w(z):
-            w_bf = keep.tile([P, N, PACK], BF16, name="w_bf%d" % z, tag="shared%d" % z, align_bytes=64)
+            w_bf = keep.tile([P, N, PACK], BF16, name="w_bf%d" % z, align_bytes=64)
             nc.scalar.copy(
                 out=w_bf[:].rearrange("p (c i) j -> p c j i", i=PACK),
                 in_=w_raw[z][:].rearrange("p j (c i) -> p c j i", i=PACK),

@@ -22,12 +22,15 @@ LANES = 16
 HALF = S // 2
 QUARTER = S // 4
 V_HALF = V // 2
+RAW_BYTES = PACK * N * 4
+REST = 64
 
 
 def tile_picked_median_none_e_kernel(tc, xT, w1, offs, pos1, pos2, pos3, out):
     nc = tc.nc
     with ExitStack() as ctx:
         keep = ctx.enter_context(tc.tile_pool(name="keep", bufs=1))
+        tied = ctx.enter_context(tc.tile_pool(name="tied", bufs=1))
         psum = ctx.enter_context(tc.psum_pool(name="psum", bufs=1))
 
         w_rows = w1.rearrange("(z p j) n -> z p j n", p=P, j=PACK)
@@ -45,7 +48,7 @@ def tile_picked_median_none_e_kernel(tc, xT, w1, offs, pos1, pos2, pos3, out):
                 nc.sync.dma_start(out=picked[:], in_=offs)
         w_raw = []
         for z in range(PASSES):
-            raw = keep.tile([P, PACK, N], F32, name="w_raw%d" % z, tag="shared%d" % z, align_bytes=64)
+            raw = tied.tile([P, PACK, N], F32, name="w_raw%d" % z, offset=z * RAW_BYTES, align_bytes=64)
             nc.sync.dma_start(out=raw[:], in_=w_rows[z])
             w_raw.append(raw)
         places = []
@@ -87,8 +90,7 @@ def tile_picked_median_none_e_kernel(tc, xT, w1, offs, pos1, pos2, pos3, out):
             nc.vector.tensor_copy(out=plain[:, j, :], in_=planes[PACK + j].indirect(picked[:]))
         nc.scalar.copy(out=x_bf[1][:, :, 0:2], in_=plain[:].rearrange("p j c -> p c j"))
         gather(1, 2, 0, S)
-        for h in range(2):
-            gather(1, PACK - 1, h * HALF, (h + 1) * HALF)
+        gather(1, PACK - 1, 0, S - REST)
 
         pieces = ((0, HALF), (HALF, HALF + QUARTER), (HALF + QUARTER, S))
         acc = [psum.tile([P, c1 - c0], F32, name="acc%d" % i) for i, (c0, c1) in enumerate(pieces)]
@@ -103,10 +105,15 @@ def tile_picked_median_none_e_kernel(tc, xT, w1, offs, pos1, pos2, pos3, out):
                 start=True,
                 stop=False,
             )
-        early_codes, early_scales = quantize(x_bf[1][:, 0:HALF, :], HALF, "x1_0", "shared0")
+        rest = tied.tile([P, REST], BF16, name="rest", offset=HALF * 4, align_bytes=64)
+        nc.vector.tensor_copy(out=rest[:], in_=planes[2 * PACK - 1].indirect(picked[:, (S - REST) // LANES : S // LANES]))
+        early_codes = tied.tile([P, HALF], U32, name="early_codes", offset=0, align_bytes=64)
+        early_scales = keep.tile([P, HALF], U8, name="early_scales", align_bytes=64)
+        nc.vector.quantize_mx(out=early_codes[:].bitcast(FP8X4), scales=early_scales[:], in_=x_bf[1][:, 0:HALF, :].rearrange("p c j -> p (c j)"))
+        nc.vector.tensor_copy(out=x_bf[1][:, S - REST : S, PACK - 1], in_=rest[:])
         x1 = [(early_codes[:], early_scales[:])]
         w1_codes, w1_scales = weave_w(1)
-        late_codes = keep.tile([P, HALF], U32, name="late_codes", tag="shared1", align_bytes=64)
+        late_codes = tied.tile([P, HALF], U32, name="late_codes", offset=RAW_BYTES, align_bytes=64)
         late_scales = keep.tile([P, HALF], U8, name="late_scales", align_bytes=64)
         for c0, c1 in pieces[1:]:
             cols = slice(c0 - HALF, c1 - HALF)

@@ -110,9 +110,9 @@ def tile_picked_median_none_e_kernel(tc, xT, w1, offs, pos1, pos2, pos3, out):
         early_codes = tied.tile([P, HALF], U32, name="early_codes", offset=0, align_bytes=64)
         early_scales = keep.tile([P, HALF], U8, name="early_scales", align_bytes=64)
         nc.vector.quantize_mx(out=early_codes[:].bitcast(FP8X4), scales=early_scales[:], in_=x_bf[1][:, 0:HALF, :].rearrange("p c j -> p (c j)"))
-        nc.vector.tensor_copy(out=x_bf[1][:, S - REST : S, PACK - 1], in_=rest[:])
         x1 = [(early_codes[:], early_scales[:])]
         w1_codes, w1_scales = weave_w(1)
+        nc.scalar.copy(out=x_bf[1][:, S - REST : S, PACK - 1], in_=rest[:])
         late_codes = tied.tile([P, HALF], U32, name="late_codes", offset=RAW_BYTES, align_bytes=64)
         late_scales = keep.tile([P, HALF], U8, name="late_scales", align_bytes=64)
         for c0, c1 in pieces[1:]:

@@ -37,13 +37,21 @@ def tile_picked_median_none_e_kernel(tc, xT, w1, offs, pos1, pos2, pos3, out):
 
         picked = keep.tile([P, S // LANES], U16, name="picked")
         x_pass = xT.rearrange("(z p j) t -> z p j t", p=P, j=PACK)
-        gap = K_PASS - (PACK - 1)
-        across = xT[PACK - 1 : PACK - 1 + 2 * gap, :].rearrange("(r q) t -> q r t", r=2)[0:gap:PACK]
-        planes = []
-        for i, src in enumerate((x_pass[0, :, 0:3, :], across, x_pass[1, :, 1:2, :], x_pass[1, :, 2:3, :], x_pass[1, :, 3:4, :])):
-            rows = keep.tile([P, src.shape[1], T], F32, name="rows%d" % i)
+        gap = K_PASS - 1
+        across = xT[K - 2 * gap : K, :].rearrange("(r q) t -> q r t", r=2)[1:gap:PACK]
+        planes = {}
+        loads = (
+            (x_pass[0, :, 0:3, :], (0, 1, 2)),
+            (across, (3, 6)),
+            (x_pass[1, :, 0:1, :], (4,)),
+            (x_pass[1, :, 1:2, :], (5,)),
+            (x_pass[1, :, 3:4, :], (7,)),
+        )
+        for i, (src, held) in enumerate(loads):
+            rows = keep.tile([P, len(held), T], F32, name="rows%d" % i)
             nc.sync.dma_start(out=rows[:], in_=src)
-            planes.extend(rows[:, j, :] for j in range(src.shape[1]))
+            for r, plane in enumerate(held):
+                planes[plane] = rows[:, r, :]
             if i == 0:
                 nc.sync.dma_start(out=picked[:], in_=offs)
         w_raw = []
@@ -84,12 +92,14 @@ def tile_picked_median_none_e_kernel(tc, xT, w1, offs, pos1, pos2, pos3, out):
             out=x_bf[0][:].rearrange("p (c i) j -> p c j i", i=PACK),
             in_=plain0[:].rearrange("p j (c i) -> p c j i", i=PACK),
         )
-        x0_codes, x0_scales = quantize(x_bf[0][:], S, "x0", "x0_codes")
-        plain = keep.tile([P, 2, S], F32, name="plain")
-        for j in range(2):
-            nc.vector.tensor_copy(out=plain[:, j, :], in_=planes[PACK + j].indirect(picked[:]))
-        nc.scalar.copy(out=x_bf[1][:, :, 0:2], in_=plain[:].rearrange("p j c -> p c j"))
         gather(1, 2, 0, S)
+        plain = keep.tile([P, 2, S], F32, name="plain")
+        nc.vector.tensor_copy(out=plain[:, 0, :], in_=planes[PACK].indirect(picked[:]))
+        x0_codes, x0_scales = quantize(x_bf[0][:], S, "x0", "x0_codes")
+        for h in range(2):
+            cols = slice(h * HALF, (h + 1) * HALF)
+            nc.vector.tensor_copy(out=plain[:, 1, cols], in_=planes[PACK + 1].indirect(picked[:, h * HALF // LANES : (h + 1) * HALF // LANES]))
+            nc.scalar.copy(out=x_bf[1][:, cols, 0:2], in_=plain[:, :, cols].rearrange("p j c -> p c j"))
         gather(1, PACK - 1, 0, S - REST)
 
         pieces = ((0, HALF), (HALF, HALF + QUARTER), (HALF + QUARTER, S))

@@ -13,6 +13,7 @@ U8 = mybir.dt.uint8
 FP8X4 = mybir.dt.float8_e4m3fn_x4
 MAX = mybir.AluOpType.max
 MIN = mybir.AluOpType.min
+COPY = mybir.ActivationFunctionType.Copy
 
 P = 128
 PACK = 4
@@ -37,14 +38,14 @@ def tile_picked_median_none_e_kernel(tc, xT, w1, offs, pos1, pos2, pos3, out):
 
         picked = keep.tile([P, S // LANES], U16, name="picked")
         x_pass = xT.rearrange("(z p j) t -> z p j t", p=P, j=PACK)
-        gap = K_PASS - 1
-        across = xT[K - 2 * gap : K, :].rearrange("(r q) t -> q r t", r=2)[1:gap:PACK]
+        gap = K_PASS - (PACK - 1)
+        across = xT[PACK - 1 : PACK - 1 + 2 * gap, :].rearrange("(r q) t -> q r t", r=2)[0:gap:PACK]
         planes = {}
         loads = (
             (x_pass[0, :, 0:3, :], (0, 1, 2)),
-            (across, (3, 6)),
-            (x_pass[1, :, 0:1, :], (4,)),
+            (across, (3, 4)),
             (x_pass[1, :, 1:2, :], (5,)),
+            (x_pass[1, :, 2:3, :], (6,)),
             (x_pass[1, :, 3:4, :], (7,)),
         )
         for i, (src, held) in enumerate(loads):
@@ -85,21 +86,20 @@ def tile_picked_median_none_e_kernel(tc, xT, w1, offs, pos1, pos2, pos3, out):
             )
             return quantize(w_bf[:], N, "w%d" % z, "w%d_codes" % z)
 
-        plain0 = keep.tile([P, PACK, S], F32, name="plain0")
-        for j in range(PACK):
+        plain0 = keep.tile([P, 2, S], F32, name="plain0")
+        for j in range(2):
             nc.vector.tensor_copy(out=plain0[:, j, :], in_=planes[j].indirect(picked[:]))
-        nc.scalar.copy(
-            out=x_bf[0][:].rearrange("p (c i) j -> p c j i", i=PACK),
-            in_=plain0[:].rearrange("p j (c i) -> p c j i", i=PACK),
-        )
-        gather(1, 2, 0, S)
-        plain = keep.tile([P, 2, S], F32, name="plain")
-        nc.vector.tensor_copy(out=plain[:, 0, :], in_=planes[PACK].indirect(picked[:]))
+        nc.scalar.copy(out=x_bf[0][:, :, 0:2], in_=plain0[:].rearrange("p j c -> p c j"))
+        gather(0, 2, 0, S)
+        gather(0, 3, 0, S)
         x0_codes, x0_scales = quantize(x_bf[0][:], S, "x0", "x0_codes")
-        for h in range(2):
-            cols = slice(h * HALF, (h + 1) * HALF)
-            nc.vector.tensor_copy(out=plain[:, 1, cols], in_=planes[PACK + 1].indirect(picked[:, h * HALF // LANES : (h + 1) * HALF // LANES]))
-            nc.scalar.copy(out=x_bf[1][:, cols, 0:2], in_=plain[:, :, cols].rearrange("p j c -> p c j"))
+        cast = keep.tile([P, T], BF16, name="cast")
+        nc.scalar.copy(out=cast[:], in_=planes[PACK])
+        nc.scalar.activation(out=x_bf[1][:, :, 0], in_=cast[:].indirect(picked[:]), func=COPY)
+        plain = keep.tile([P, S], F32, name="plain")
+        nc.vector.tensor_copy(out=plain[:], in_=planes[PACK + 1].indirect(picked[:]))
+        nc.scalar.copy(out=x_bf[1][:, :, 1], in_=plain[:])
+        gather(1, 2, 0, S)
         gather(1, PACK - 1, 0, S - REST)
 
         pieces = ((0, HALF), (HALF, HALF + QUARTER), (HALF + QUARTER, S))

@@ -25,6 +25,7 @@ QUARTER = S // 4
 V_HALF = V // 2
 RAW_BYTES = PACK * N * 4
 REST = 64
+CAST_V = 32
 
 
 def tile_picked_median_none_e_kernel(tc, xT, w1, offs, pos1, pos2, pos3, out):
@@ -38,13 +39,10 @@ def tile_picked_median_none_e_kernel(tc, xT, w1, offs, pos1, pos2, pos3, out):
 
         picked = keep.tile([P, S // LANES], U16, name="picked")
         x_pass = xT.rearrange("(z p j) t -> z p j t", p=P, j=PACK)
-        gap = K_PASS - (PACK - 1)
-        across = xT[PACK - 1 : PACK - 1 + 2 * gap, :].rearrange("(r q) t -> q r t", r=2)[0:gap:PACK]
         planes = {}
         loads = (
-            (x_pass[0, :, 0:3, :], (0, 1, 2)),
-            (across, (3, 4)),
-            (x_pass[1, :, 1:2, :], (5,)),
+            (x_pass[0], (0, 1, 2, 3)),
+            (x_pass[1, :, 0:2, :], (4, 5)),
             (x_pass[1, :, 2:3, :], (6,)),
             (x_pass[1, :, 3:4, :], (7,)),
         )
@@ -86,19 +84,29 @@ def tile_picked_median_none_e_kernel(tc, xT, w1, offs, pos1, pos2, pos3, out):
             )
             return quantize(w_bf[:], N, "w%d" % z, "w%d_codes" % z)
 
-        plain0 = keep.tile([P, 2, S], F32, name="plain0")
-        for j in range(2):
-            nc.vector.tensor_copy(out=plain0[:, j, :], in_=planes[j].indirect(picked[:]))
-        nc.scalar.copy(out=x_bf[0][:, :, 0:2], in_=plain0[:].rearrange("p j c -> p c j"))
+        casts = [keep.tile([P, T], BF16, name="cast%d" % z) for z in range(PASSES)]
+
+        def first_plane(z, lo, hi):
+            nc.scalar.activation(out=x_bf[z][:, lo:hi, 0], in_=casts[z][:].indirect(picked[:, lo // LANES : hi // LANES]), func=COPY)
+
+        nc.scalar.copy(out=casts[0][:], in_=planes[0])
+        gather(0, 1, 0, HALF)
+        plain = keep.tile([P, HALF], F32, name="plain")
+        nc.vector.tensor_copy(out=plain[:], in_=planes[1].indirect(picked[:, HALF // LANES : S // LANES]))
+        nc.scalar.copy(out=x_bf[0][:, HALF:S, 1], in_=plain[:])
         gather(0, 2, 0, S)
-        gather(0, 3, 0, S)
-        x0_codes, x0_scales = quantize(x_bf[0][:], S, "x0", "x0_codes")
-        cast = keep.tile([P, T], BF16, name="cast")
-        nc.scalar.copy(out=cast[:], in_=planes[PACK])
-        nc.scalar.activation(out=x_bf[1][:, :, 0], in_=cast[:].indirect(picked[:]), func=COPY)
-        plain = keep.tile([P, S], F32, name="plain")
-        nc.vector.tensor_copy(out=plain[:], in_=planes[PACK + 1].indirect(picked[:]))
-        nc.scalar.copy(out=x_bf[1][:, :, 1], in_=plain[:])
+        x0_codes = keep.tile([P, S], U32, name="x0_codes", align_bytes=64)
+        x0_scales = keep.tile([P, S], U8, name="x0_scales", align_bytes=64)
+        for h in range(2):
+            first_plane(0, h * HALF, (h + 1) * HALF)
+            gather(0, 3, h * HALF, (h + 1) * HALF)
+        for h in range(2):
+            cols = slice(h * HALF, (h + 1) * HALF)
+            nc.vector.quantize_mx(out=x0_codes[:, cols].bitcast(FP8X4), scales=x0_scales[:, cols], in_=x_bf[0][:, cols, :].rearrange("p c j -> p (c j)"))
+        gather(1, 1, 0, S)
+        nc.vector.tensor_copy(out=casts[1][:, T - CAST_V :], in_=planes[PACK][:, T - CAST_V :])
+        nc.scalar.copy(out=casts[1][:, : T - CAST_V], in_=planes[PACK][:, : T - CAST_V])
+        first_plane(1, 0, S)
         gather(1, 2, 0, S)
         gather(1, PACK - 1, 0, S - REST)
 

@@ -26,6 +26,7 @@ V_HALF = V // 2
 RAW_BYTES = PACK * N * 4
 REST = 64
 CAST_V = 32
+CAST_0 = 256
 
 
 def tile_picked_median_none_e_kernel(tc, xT, w1, offs, pos1, pos2, pos3, out):
@@ -38,6 +39,7 @@ def tile_picked_median_none_e_kernel(tc, xT, w1, offs, pos1, pos2, pos3, out):
         w_rows = w1.rearrange("(z p j) n -> z p j n", p=P, j=PACK)
 
         picked = keep.tile([P, S // LANES], U16, name="picked")
+        nc.sync.dma_start(out=picked[:], in_=offs)
         x_pass = xT.rearrange("(z p j) t -> z p j t", p=P, j=PACK)
         planes = {}
         loads = (
@@ -51,8 +53,6 @@ def tile_picked_median_none_e_kernel(tc, xT, w1, offs, pos1, pos2, pos3, out):
             nc.sync.dma_start(out=rows[:], in_=src)
             for r, plane in enumerate(held):
                 planes[plane] = rows[:, r, :]
-            if i == 0:
-                nc.sync.dma_start(out=picked[:], in_=offs)
         w_raw = []
         for z in range(PASSES):
             raw = tied.tile([P, PACK, N], F32, name="w_raw%d" % z, offset=z * RAW_BYTES, align_bytes=64)
@@ -64,7 +64,7 @@ def tile_picked_median_none_e_kernel(tc, xT, w1, offs, pos1, pos2, pos3, out):
             nc.sync.dma_start(out=place[:], in_=pos)
             places.append(place)
 
-        x_bf = [keep.tile([P, S, PACK], BF16, name="x_bf%d" % z, align_bytes=64) for z in range(PASSES)]
+        x_bf = {1: keep.tile([P, S, PACK], BF16, name="x_bf1", align_bytes=64)}
 
         def gather(z, j, lo, hi):
             window = planes[z * PACK + j]
@@ -89,20 +89,30 @@ def tile_picked_median_none_e_kernel(tc, xT, w1, offs, pos1, pos2, pos3, out):
         def first_plane(z, lo, hi):
             nc.scalar.activation(out=x_bf[z][:, lo:hi, 0], in_=casts[z][:].indirect(picked[:, lo // LANES : hi // LANES]), func=COPY)
 
-        nc.scalar.copy(out=casts[0][:], in_=planes[0])
-        gather(0, 1, 0, HALF)
-        plain = keep.tile([P, HALF], F32, name="plain")
-        nc.vector.tensor_copy(out=plain[:], in_=planes[1].indirect(picked[:, HALF // LANES : S // LANES]))
-        nc.scalar.copy(out=x_bf[0][:, HALF:S, 1], in_=plain[:])
-        gather(0, 2, 0, S)
+        pairs = [keep.tile([P, 2, HALF, 2], BF16, name="pairs%d" % h) for h in range(2)]
+        halves = [picked[:, h * HALF // LANES : (h + 1) * HALF // LANES] for h in range(2)]
+
+        def gather_pair(h, j):
+            nc.vector.tensor_copy(out=pairs[h][:, j // 2, :, j % 2], in_=planes[j].indirect(halves[h]))
+
+        for h in range(2):
+            gather_pair(h, 1)
+        nc.vector.tensor_copy(out=casts[0][:, T - CAST_0 :], in_=planes[0][:, T - CAST_0 :])
+        nc.scalar.copy(out=casts[0][:, : T - CAST_0], in_=planes[0][:, : T - CAST_0])
+        for h in range(2):
+            nc.scalar.activation(out=pairs[h][:, 0, :, 0], in_=casts[0][:].indirect(halves[h]), func=COPY)
+            gather_pair(h, 2)
+            gather_pair(h, 3)
         x0_codes = keep.tile([P, S], U32, name="x0_codes", align_bytes=64)
         x0_scales = keep.tile([P, S], U8, name="x0_scales", align_bytes=64)
         for h in range(2):
-            first_plane(0, h * HALF, (h + 1) * HALF)
-            gather(0, 3, h * HALF, (h + 1) * HALF)
-        for h in range(2):
             cols = slice(h * HALF, (h + 1) * HALF)
-            nc.vector.quantize_mx(out=x0_codes[:, cols].bitcast(FP8X4), scales=x0_scales[:, cols], in_=x_bf[0][:, cols, :].rearrange("p c j -> p (c j)"))
+            woven = keep.tile([P, HALF * PACK], BF16, name="woven%d" % h, align_bytes=64)
+            nc.scalar.copy(
+                out=woven[:].bitcast(U32).rearrange("p (c i u) -> p c u i", i=PACK, u=2),
+                in_=pairs[h][:].rearrange("p u c e -> p (u c e)").bitcast(U32).rearrange("p (u c i) -> p c u i", i=PACK, u=2),
+            )
+            nc.vector.quantize_mx(out=x0_codes[:, cols].bitcast(FP8X4), scales=x0_scales[:, cols], in_=woven[:])
         gather(1, 1, 0, S)
         nc.vector.tensor_copy(out=casts[1][:, T - CAST_V :], in_=planes[PACK][:, T - CAST_V :])
         nc.scalar.copy(out=casts[1][:, : T - CAST_V], in_=planes[PACK][:, : T - CAST_V])

@@ -25,6 +25,7 @@ QUARTER = S // 4
 V_HALF = V // 2
 RAW_BYTES = PACK * N * 4
 REST = 64
+V_LAST = 64
 CAST_V = 32
 CAST_0 = 256
 
@@ -175,14 +176,17 @@ def tile_picked_median_none_e_kernel(tc, xT, w1, offs, pos1, pos2, pos3, out):
             near.append(got)
         hi = keep.tile([P, V], F32, name="hi")
         lo = keep.tile([P, V], F32, name="lo")
-        nc.vector.tensor_tensor(out=hi[:], in0=near[0][:], in1=near[1][:], op=MAX)
-        nc.vector.tensor_tensor(out=lo[:], in0=near[0][:], in1=near[1][:], op=MIN)
         capped = keep.tile([P, V], F32, name="capped")
+        meds = [keep.tile([P, V_HALF], F32, name="med%d" % h) for h in range(2)]
+        most, last = slice(0, V - V_LAST), slice(V - V_LAST, V)
+        nc.vector.tensor_tensor(out=hi[:], in0=near[0][:], in1=near[1][:], op=MAX)
+        nc.vector.tensor_tensor(out=lo[:, most], in0=near[0][:, most], in1=near[1][:, most], op=MIN)
         for h in range(2):
             cols = slice(h * V_HALF, (h + 1) * V_HALF)
             nc.vector.tensor_tensor(out=capped[:, cols], in0=hi[:, cols], in1=near[2][:, cols], op=MIN)
-        for h in range(2):
-            cols = slice(h * V_HALF, (h + 1) * V_HALF)
-            med = keep.tile([P, V_HALF], F32, name="med%d" % h)
-            nc.vector.tensor_tensor(out=med[:], in0=lo[:, cols], in1=capped[:, cols], op=MAX)
-            nc.sync.dma_start(out=out[:, cols], in_=med[:])
+        nc.vector.tensor_tensor(out=lo[:, last], in0=near[0][:, last], in1=near[1][:, last], op=MIN)
+        nc.vector.tensor_tensor(out=meds[0][:], in0=lo[:, 0:V_HALF], in1=capped[:, 0:V_HALF], op=MAX)
+        nc.sync.dma_start(out=out[:, 0:V_HALF], in_=meds[0][:])
+        for c0, c1 in ((V_HALF, V - V_LAST), (V - V_LAST, V)):
+            nc.vector.tensor_tensor(out=meds[1][:, c0 - V_HALF : c1 - V_HALF], in0=lo[:, c0:c1], in1=capped[:, c0:c1], op=MAX)
+        nc.sync.dma_start(out=out[:, V_HALF:V], in_=meds[1][:])

@@ -25,7 +25,6 @@ QUARTER = S // 4
 V_HALF = V // 2
 RAW_BYTES = PACK * N * 4
 REST = 64
-V_LAST = 64
 CAST_V = 32
 CAST_0 = 256
 
@@ -169,24 +168,20 @@ def tile_picked_median_none_e_kernel(tc, xT, w1, offs, pos1, pos2, pos3, out):
             else:
                 nc.scalar.copy(out=y[:, c0:c1], in_=acc[i][:])
 
-        near = []
-        for d in range(3):
-            got = keep.tile([P, V], F32, name="near%d" % d)
-            nc.vector.tensor_copy(out=got[:], in_=y[:].indirect(places[d][:]))
-            near.append(got)
+        near = [keep.tile([P, V], F32, name="near%d" % d) for d in range(3)]
+        v_halves = [slice(h * V_HALF, (h + 1) * V_HALF) for h in range(2)]
+        nc.vector.tensor_copy(out=near[0][:], in_=y[:].indirect(places[0][:]))
+        nc.scalar.activation(out=near[1][:], in_=y[:].indirect(places[1][:]), func=COPY)
+        for cols in v_halves:
+            nc.scalar.activation(out=near[2][:, cols], in_=y[:].indirect(places[2][:, cols.start // LANES : cols.stop // LANES]), func=COPY)
         hi = keep.tile([P, V], F32, name="hi")
         lo = keep.tile([P, V], F32, name="lo")
         capped = keep.tile([P, V], F32, name="capped")
         meds = [keep.tile([P, V_HALF], F32, name="med%d" % h) for h in range(2)]
-        most, last = slice(0, V - V_LAST), slice(V - V_LAST, V)
         nc.vector.tensor_tensor(out=hi[:], in0=near[0][:], in1=near[1][:], op=MAX)
-        nc.vector.tensor_tensor(out=lo[:, most], in0=near[0][:, most], in1=near[1][:, most], op=MIN)
-        for h in range(2):
-            cols = slice(h * V_HALF, (h + 1) * V_HALF)
+        nc.vector.tensor_tensor(out=lo[:], in0=near[0][:], in1=near[1][:], op=MIN)
+        for cols in v_halves:
             nc.vector.tensor_tensor(out=capped[:, cols], in0=hi[:, cols], in1=near[2][:, cols], op=MIN)
-        nc.vector.tensor_tensor(out=lo[:, last], in0=near[0][:, last], in1=near[1][:, last], op=MIN)
-        nc.vector.tensor_tensor(out=meds[0][:], in0=lo[:, 0:V_HALF], in1=capped[:, 0:V_HALF], op=MAX)
-        nc.sync.dma_start(out=out[:, 0:V_HALF], in_=meds[0][:])
-        for c0, c1 in ((V_HALF, V - V_LAST), (V - V_LAST, V)):
-            nc.vector.tensor_tensor(out=meds[1][:, c0 - V_HALF : c1 - V_HALF], in0=lo[:, c0:c1], in1=capped[:, c0:c1], op=MAX)
-        nc.sync.dma_start(out=out[:, V_HALF:V], in_=meds[1][:])
+        for h, cols in enumerate(v_halves):
+            nc.vector.tensor_tensor(out=meds[h][:], in0=lo[:, cols], in1=capped[:, cols], op=MAX)
+            nc.sync.dma_start(out=out[:, cols], in_=meds[h][:])

@@ -25,8 +25,7 @@ QUARTER = S // 4
 V_HALF = V // 2
 RAW_BYTES = PACK * N * 4
 REST = 64
-CAST_V = 32
-CAST_0 = 256
+V_LAST = 64
 
 
 def tile_picked_median_none_e_kernel(tc, xT, w1, offs, pos1, pos2, pos3, out):
@@ -39,7 +38,6 @@ def tile_picked_median_none_e_kernel(tc, xT, w1, offs, pos1, pos2, pos3, out):
         w_rows = w1.rearrange("(z p j) n -> z p j n", p=P, j=PACK)
 
         picked = keep.tile([P, S // LANES], U16, name="picked")
-        nc.sync.dma_start(out=picked[:], in_=offs)
         x_pass = xT.rearrange("(z p j) t -> z p j t", p=P, j=PACK)
         planes = {}
         loads = (
@@ -51,6 +49,8 @@ def tile_picked_median_none_e_kernel(tc, xT, w1, offs, pos1, pos2, pos3, out):
         for i, (src, held) in enumerate(loads):
             rows = keep.tile([P, len(held), T], F32, name="rows%d" % i)
             nc.sync.dma_start(out=rows[:], in_=src)
+            if i == 0:
+                nc.sync.dma_start(out=picked[:], in_=offs)
             for r, plane in enumerate(held):
                 planes[plane] = rows[:, r, :]
         w_raw = []
@@ -84,39 +84,26 @@ def tile_picked_median_none_e_kernel(tc, xT, w1, offs, pos1, pos2, pos3, out):
             )
             return quantize(w_bf[:], N, "w%d" % z, "w%d_codes" % z)
 
-        casts = [keep.tile([P, T], BF16, name="cast%d" % z) for z in range(PASSES)]
-
-        def first_plane(z, lo, hi):
-            nc.scalar.activation(out=x_bf[z][:, lo:hi, 0], in_=casts[z][:].indirect(picked[:, lo // LANES : hi // LANES]), func=COPY)
-
-        pairs = [keep.tile([P, 2, HALF, 2], BF16, name="pairs%d" % h) for h in range(2)]
         halves = [picked[:, h * HALF // LANES : (h + 1) * HALF // LANES] for h in range(2)]
-
-        def gather_pair(h, j):
-            nc.vector.tensor_copy(out=pairs[h][:, j // 2, :, j % 2], in_=planes[j].indirect(halves[h]))
-
-        for h in range(2):
-            gather_pair(h, 1)
-        nc.vector.tensor_copy(out=casts[0][:, T - CAST_0 :], in_=planes[0][:, T - CAST_0 :])
-        nc.scalar.copy(out=casts[0][:, : T - CAST_0], in_=planes[0][:, : T - CAST_0])
-        for h in range(2):
-            nc.scalar.activation(out=pairs[h][:, 0, :, 0], in_=casts[0][:].indirect(halves[h]), func=COPY)
-            gather_pair(h, 2)
-            gather_pair(h, 3)
         x0_codes = keep.tile([P, S], U32, name="x0_codes", align_bytes=64)
         x0_scales = keep.tile([P, S], U8, name="x0_scales", align_bytes=64)
+        runs = [keep.tile([P, PACK, HALF], F32, name="runs%d" % h) for h in range(2)]
+        for h in range(2):
+            for j in range(2):
+                nc.scalar.activation(out=runs[h][:, j, :], in_=planes[j].indirect(halves[h]), func=COPY)
+                nc.vector.tensor_copy(out=runs[h][:, 2 + j, :], in_=planes[2 + j].indirect(halves[h]))
         for h in range(2):
             cols = slice(h * HALF, (h + 1) * HALF)
-            woven = keep.tile([P, HALF * PACK], BF16, name="woven%d" % h, align_bytes=64)
-            nc.scalar.copy(
-                out=woven[:].bitcast(U32).rearrange("p (c i u) -> p c u i", i=PACK, u=2),
-                in_=pairs[h][:].rearrange("p u c e -> p (u c e)").bitcast(U32).rearrange("p (u c i) -> p c u i", i=PACK, u=2),
+            woven = keep.tile([P, HALF, PACK], BF16, name="woven%d" % h, align_bytes=64)
+            nc.vector.tensor_copy(
+                out=woven[:].rearrange("p (c i) j -> p c j i", i=PACK),
+                in_=runs[h][:].rearrange("p j (c i) -> p c j i", i=PACK),
             )
-            nc.vector.quantize_mx(out=x0_codes[:, cols].bitcast(FP8X4), scales=x0_scales[:, cols], in_=woven[:])
-        gather(1, 1, 0, S)
-        nc.vector.tensor_copy(out=casts[1][:, T - CAST_V :], in_=planes[PACK][:, T - CAST_V :])
-        nc.scalar.copy(out=casts[1][:, : T - CAST_V], in_=planes[PACK][:, : T - CAST_V])
-        first_plane(1, 0, S)
+            nc.vector.quantize_mx(out=x0_codes[:, cols].bitcast(FP8X4), scales=x0_scales[:, cols], in_=woven[:].rearrange("p c j -> p (c j)"))
+        pair = keep.tile([P, 2, S], F32, name="pair")
+        nc.scalar.activation(out=pair[:, 0, :], in_=planes[PACK].indirect(picked[:]), func=COPY)
+        nc.vector.tensor_copy(out=pair[:, 1, :], in_=planes[PACK + 1].indirect(picked[:]))
+        nc.scalar.copy(out=x_bf[1][:, :, 0:2], in_=pair[:].rearrange("p j c -> p c j"))
         gather(1, 2, 0, S)
         gather(1, PACK - 1, 0, S - REST)
 
@@ -169,19 +156,27 @@ def tile_picked_median_none_e_kernel(tc, xT, w1, offs, pos1, pos2, pos3, out):
                 nc.scalar.copy(out=y[:, c0:c1], in_=acc[i][:])
 
         near = [keep.tile([P, V], F32, name="near%d" % d) for d in range(3)]
-        v_halves = [slice(h * V_HALF, (h + 1) * V_HALF) for h in range(2)]
-        nc.vector.tensor_copy(out=near[0][:], in_=y[:].indirect(places[0][:]))
-        nc.scalar.activation(out=near[1][:], in_=y[:].indirect(places[1][:]), func=COPY)
-        for cols in v_halves:
-            nc.scalar.activation(out=near[2][:, cols], in_=y[:].indirect(places[2][:, cols.start // LANES : cols.stop // LANES]), func=COPY)
+        first, second = slice(0, V_HALF), slice(V_HALF, V)
+        third, fourth = slice(V_HALF, V - V_LAST), slice(V - V_LAST, V)
+
+        def neighbours(d, cols):
+            return y[:].indirect(places[d][:, cols.start // LANES : cols.stop // LANES])
+
+        for cols in (first, second):
+            nc.vector.tensor_copy(out=near[0][:, cols], in_=neighbours(0, cols))
+            nc.scalar.activation(out=near[1][:, cols], in_=neighbours(1, cols), func=COPY)
+        for cols in (first, third, fourth):
+            nc.scalar.activation(out=near[2][:, cols], in_=neighbours(2, cols), func=COPY)
         hi = keep.tile([P, V], F32, name="hi")
         lo = keep.tile([P, V], F32, name="lo")
         capped = keep.tile([P, V], F32, name="capped")
-        meds = [keep.tile([P, V_HALF], F32, name="med%d" % h) for h in range(2)]
-        nc.vector.tensor_tensor(out=hi[:], in0=near[0][:], in1=near[1][:], op=MAX)
-        nc.vector.tensor_tensor(out=lo[:], in0=near[0][:], in1=near[1][:], op=MIN)
-        for cols in v_halves:
+        med = keep.tile([P, V], F32, name="med")
+        for cols in (first, second):
+            nc.vector.tensor_tensor(out=hi[:, cols], in0=near[0][:, cols], in1=near[1][:, cols], op=MAX)
+            nc.vector.tensor_tensor(out=lo[:, cols], in0=near[0][:, cols], in1=near[1][:, cols], op=MIN)
+        for cols in (first, third, fourth):
             nc.vector.tensor_tensor(out=capped[:, cols], in0=hi[:, cols], in1=near[2][:, cols], op=MIN)
-        for h, cols in enumerate(v_halves):
-            nc.vector.tensor_tensor(out=meds[h][:], in0=lo[:, cols], in1=capped[:, cols], op=MAX)
-            nc.sync.dma_start(out=out[:, cols], in_=meds[h][:])
+        for cols in (first, third, fourth):
+            nc.vector.tensor_tensor(out=med[:, cols], in0=lo[:, cols], in1=capped[:, cols], op=MAX)
+        for cols in (first, second):
+            nc.sync.dma_start(out=out[:, cols], in_=med[:, cols])

@@ -76,12 +76,13 @@ def tile_picked_median_none_e_kernel(tc, xT, w1, offs, pos1, pos2, pos3, out):
             nc.vector.quantize_mx(out=codes[:].bitcast(FP8X4), scales=scales[:], in_=src.rearrange("p c j -> p (c j)"))
             return codes, scales
 
-        def weave_w(z):
+        def weave_w(z, shares):
             w_bf = keep.tile([P, N, PACK], BF16, name="w_bf%d" % z, align_bytes=64)
-            nc.scalar.copy(
-                out=w_bf[:].rearrange("p (c i) j -> p c j i", i=PACK),
-                in_=w_raw[z][:].rearrange("p j (c i) -> p c j i", i=PACK),
-            )
+            for copy, cols in shares:
+                copy(
+                    out=w_bf[:, cols, :].rearrange("p (c i) j -> p c j i", i=PACK),
+                    in_=w_raw[z][:, :, cols].rearrange("p j (c i) -> p c j i", i=PACK),
+                )
             return quantize(w_bf[:], N, "w%d" % z, "w%d_codes" % z)
 
         halves = [picked[:, h * HALF // LANES : (h + 1) * HALF // LANES] for h in range(2)]
@@ -105,11 +106,14 @@ def tile_picked_median_none_e_kernel(tc, xT, w1, offs, pos1, pos2, pos3, out):
         nc.vector.tensor_copy(out=pair[:, 1, :], in_=planes[PACK + 1].indirect(picked[:]))
         nc.scalar.copy(out=x_bf[1][:, :, 0:2], in_=pair[:].rearrange("p j c -> p c j"))
         gather(1, 2, 0, S)
-        gather(1, PACK - 1, 0, S - REST)
+        middle = keep.tile([P, HALF - REST], BF16, name="middle")
+        nc.scalar.activation(out=middle[:], in_=planes[2 * PACK - 1].indirect(picked[:, HALF // LANES : (S - REST) // LANES]), func=COPY)
+        gather(1, PACK - 1, 0, HALF)
+        nc.vector.tensor_copy(out=x_bf[1][:, HALF : S - REST, PACK - 1], in_=middle[:])
 
         pieces = ((0, HALF), (HALF, HALF + QUARTER), (HALF + QUARTER, S))
         acc = [psum.tile([P, c1 - c0], F32, name="acc%d" % i) for i, (c0, c1) in enumerate(pieces)]
-        w0_codes, w0_scales = weave_w(0)
+        w0_codes, w0_scales = weave_w(0, ((nc.scalar.copy, slice(0, N)),))
         for i, (c0, c1) in enumerate(pieces):
             nc.tensor.matmul_mx(
                 out=acc[i][:],
@@ -126,7 +130,7 @@ def tile_picked_median_none_e_kernel(tc, xT, w1, offs, pos1, pos2, pos3, out):
         early_scales = keep.tile([P, HALF], U8, name="early_scales", align_bytes=64)
         nc.vector.quantize_mx(out=early_codes[:].bitcast(FP8X4), scales=early_scales[:], in_=x_bf[1][:, 0:HALF, :].rearrange("p c j -> p (c j)"))
         x1 = [(early_codes[:], early_scales[:])]
-        w1_codes, w1_scales = weave_w(1)
+        w1_codes, w1_scales = weave_w(1, ((nc.scalar.copy, slice(0, N // 2)), (nc.vector.tensor_copy, slice(N // 2, N))))
         nc.scalar.copy(out=x_bf[1][:, S - REST : S, PACK - 1], in_=rest[:])
         late_codes = tied.tile([P, HALF], U32, name="late_codes", offset=RAW_BYTES, align_bytes=64)
         late_scales = keep.tile([P, HALF], U8, name="late_scales", align_bytes=64)

@@ -26,6 +26,8 @@ V_HALF = V // 2
 RAW_BYTES = PACK * N * 4
 REST = 64
 V_LAST = 64
+STEPPED = 352
+W_SCALAR = 80
 
 
 def tile_picked_median_none_e_kernel(tc, xT, w1, offs, pos1, pos2, pos3, out):
@@ -106,10 +108,10 @@ def tile_picked_median_none_e_kernel(tc, xT, w1, offs, pos1, pos2, pos3, out):
         nc.vector.tensor_copy(out=pair[:, 1, :], in_=planes[PACK + 1].indirect(picked[:]))
         nc.scalar.copy(out=x_bf[1][:, :, 0:2], in_=pair[:].rearrange("p j c -> p c j"))
         gather(1, 2, 0, S)
-        middle = keep.tile([P, HALF - REST], BF16, name="middle")
-        nc.scalar.activation(out=middle[:], in_=planes[2 * PACK - 1].indirect(picked[:, HALF // LANES : (S - REST) // LANES]), func=COPY)
-        gather(1, PACK - 1, 0, HALF)
-        nc.vector.tensor_copy(out=x_bf[1][:, HALF : S - REST, PACK - 1], in_=middle[:])
+        middle = keep.tile([P, S - REST - STEPPED], BF16, name="middle")
+        nc.scalar.activation(out=middle[:], in_=planes[2 * PACK - 1].indirect(picked[:, STEPPED // LANES : (S - REST) // LANES]), func=COPY)
+        gather(1, PACK - 1, 0, STEPPED)
+        nc.vector.tensor_copy(out=x_bf[1][:, STEPPED : S - REST, PACK - 1], in_=middle[:])
 
         pieces = ((0, HALF), (HALF, HALF + QUARTER), (HALF + QUARTER, S))
         acc = [psum.tile([P, c1 - c0], F32, name="acc%d" % i) for i, (c0, c1) in enumerate(pieces)]
@@ -130,7 +132,7 @@ def tile_picked_median_none_e_kernel(tc, xT, w1, offs, pos1, pos2, pos3, out):
         early_scales = keep.tile([P, HALF], U8, name="early_scales", align_bytes=64)
         nc.vector.quantize_mx(out=early_codes[:].bitcast(FP8X4), scales=early_scales[:], in_=x_bf[1][:, 0:HALF, :].rearrange("p c j -> p (c j)"))
         x1 = [(early_codes[:], early_scales[:])]
-        w1_codes, w1_scales = weave_w(1, ((nc.scalar.copy, slice(0, N // 2)), (nc.vector.tensor_copy, slice(N // 2, N))))
+        w1_codes, w1_scales = weave_w(1, ((nc.scalar.copy, slice(0, W_SCALAR)), (nc.vector.tensor_copy, slice(W_SCALAR, N))))
         nc.scalar.copy(out=x_bf[1][:, S - REST : S, PACK - 1], in_=rest[:])
         late_codes = tied.tile([P, HALF], U32, name="late_codes", offset=RAW_BYTES, align_bytes=64)
         late_scales = keep.tile([P, HALF], U8, name="late_scales", align_bytes=64)
@@ -169,7 +171,8 @@ def tile_picked_median_none_e_kernel(tc, xT, w1, offs, pos1, pos2, pos3, out):
         for cols in (first, second):
             nc.vector.tensor_copy(out=near[0][:, cols], in_=neighbours(0, cols))
             nc.scalar.activation(out=near[1][:, cols], in_=neighbours(1, cols), func=COPY)
-        for cols in (first, third, fourth):
+        nc.vector.tensor_copy(out=near[2][:, fourth], in_=neighbours(2, fourth))
+        for cols in (first, third):
             nc.scalar.activation(out=near[2][:, cols], in_=neighbours(2, cols), func=COPY)
         hi = keep.tile([P, V], F32, name="hi")
         lo = keep.tile([P, V], F32, name="lo")
@@ -178,9 +181,9 @@ def tile_picked_median_none_e_kernel(tc, xT, w1, offs, pos1, pos2, pos3, out):
         for cols in (first, second):
             nc.vector.tensor_tensor(out=hi[:, cols], in0=near[0][:, cols], in1=near[1][:, cols], op=MAX)
             nc.vector.tensor_tensor(out=lo[:, cols], in0=near[0][:, cols], in1=near[1][:, cols], op=MIN)
-        for cols in (first, third, fourth):
+        for cols in (fourth, first, third):
             nc.vector.tensor_tensor(out=capped[:, cols], in0=hi[:, cols], in1=near[2][:, cols], op=MIN)
-        for cols in (first, third, fourth):
+        for cols in (first, fourth, third):
             nc.vector.tensor_tensor(out=med[:, cols], in0=lo[:, cols], in1=capped[:, cols], op=MAX)
         for cols in (first, second):
             nc.sync.dma_start(out=out[:, cols], in_=med[:, cols])

@@ -21,13 +21,12 @@ K_PASS = P * PACK
 PASSES = K // K_PASS
 LANES = 16
 HALF = S // 2
-QUARTER = S // 4
+PIECE = 128
+PIECES = S // PIECE
 V_HALF = V // 2
-RAW_BYTES = PACK * N * 4
-REST = 64
 V_LAST = 64
-STEPPED = 352
-W_SCALAR = 80
+RAW_BYTES = PACK * N * 4
+W1_SCALAR = 64
 
 
 def tile_picked_median_none_e_kernel(tc, xT, w1, offs, pos1, pos2, pos3, out):
@@ -37,28 +36,21 @@ def tile_picked_median_none_e_kernel(tc, xT, w1, offs, pos1, pos2, pos3, out):
         tied = ctx.enter_context(tc.tile_pool(name="tied", bufs=1))
         psum = ctx.enter_context(tc.psum_pool(name="psum", bufs=1))
 
-        w_rows = w1.rearrange("(z p j) n -> z p j n", p=P, j=PACK)
-
         picked = keep.tile([P, S // LANES], U16, name="picked")
         x_pass = xT.rearrange("(z p j) t -> z p j t", p=P, j=PACK)
+        w_pass = w1.rearrange("(z p j) n -> z p j n", p=P, j=PACK)
         planes = {}
-        loads = (
-            (x_pass[0], (0, 1, 2, 3)),
-            (x_pass[1, :, 0:2, :], (4, 5)),
-            (x_pass[1, :, 2:3, :], (6,)),
-            (x_pass[1, :, 3:4, :], (7,)),
-        )
-        for i, (src, held) in enumerate(loads):
-            rows = keep.tile([P, len(held), T], F32, name="rows%d" % i)
-            nc.sync.dma_start(out=rows[:], in_=src)
+        for i, (z, j0, j1) in enumerate(((0, 0, 4), (1, 0, 2), (1, 2, 3), (1, 3, 4))):
+            rows = keep.tile([P, j1 - j0, T], F32, name="rows%d" % i)
+            nc.sync.dma_start(out=rows[:], in_=x_pass[z, :, j0:j1, :])
             if i == 0:
                 nc.sync.dma_start(out=picked[:], in_=offs)
-            for r, plane in enumerate(held):
-                planes[plane] = rows[:, r, :]
+            for j in range(j0, j1):
+                planes[z, j] = rows[:, j - j0, :]
         w_raw = []
         for z in range(PASSES):
             raw = tied.tile([P, PACK, N], F32, name="w_raw%d" % z, offset=z * RAW_BYTES, align_bytes=64)
-            nc.sync.dma_start(out=raw[:], in_=w_rows[z])
+            nc.sync.dma_start(out=raw[:], in_=w_pass[z])
             w_raw.append(raw)
         places = []
         for d, pos in enumerate((pos1, pos2, pos3)):
@@ -66,100 +58,85 @@ def tile_picked_median_none_e_kernel(tc, xT, w1, offs, pos1, pos2, pos3, out):
             nc.sync.dma_start(out=place[:], in_=pos)
             places.append(place)
 
-        x_bf = {1: keep.tile([P, S, PACK], BF16, name="x_bf1", align_bytes=64)}
+        def nodes(z, j, lo, hi):
+            return planes[z, j].indirect(picked[:, lo // LANES : hi // LANES])
 
-        def gather(z, j, lo, hi):
-            window = planes[z * PACK + j]
-            nc.vector.tensor_copy(out=x_bf[z][:, lo:hi, j], in_=window.indirect(picked[:, lo // LANES : hi // LANES]))
+        def scalar_gather(out, in_):
+            nc.scalar.activation(out=out, in_=in_, func=COPY)
 
-        def quantize(src, width, name, tag):
-            codes = keep.tile([P, width], U32, name=name + "_codes", tag=tag, align_bytes=64)
-            scales = keep.tile([P, width], U8, name=name + "_scales", align_bytes=64)
-            nc.vector.quantize_mx(out=codes[:].bitcast(FP8X4), scales=scales[:], in_=src.rearrange("p c j -> p (c j)"))
-            return codes, scales
+        def weave(copy, woven, raw, cols):
+            copy(
+                out=woven[:, cols, :].rearrange("p (c i) j -> p c j i", i=PACK),
+                in_=raw[:, :, cols].rearrange("p j (c i) -> p c j i", i=PACK),
+            )
 
-        def weave_w(z, shares):
-            w_bf = keep.tile([P, N, PACK], BF16, name="w_bf%d" % z, align_bytes=64)
-            for copy, cols in shares:
-                copy(
-                    out=w_bf[:, cols, :].rearrange("p (c i) j -> p c j i", i=PACK),
-                    in_=w_raw[z][:, :, cols].rearrange("p j (c i) -> p c j i", i=PACK),
-                )
-            return quantize(w_bf[:], N, "w%d" % z, "w%d_codes" % z)
+        def quantize(codes, scales, woven):
+            nc.vector.quantize_mx(out=codes.bitcast(FP8X4), scales=scales, in_=woven.rearrange("p c j -> p (c j)"))
 
-        halves = [picked[:, h * HALF // LANES : (h + 1) * HALF // LANES] for h in range(2)]
         x0_codes = keep.tile([P, S], U32, name="x0_codes", align_bytes=64)
         x0_scales = keep.tile([P, S], U8, name="x0_scales", align_bytes=64)
         runs = [keep.tile([P, PACK, HALF], F32, name="runs%d" % h) for h in range(2)]
+        for h, scalar_planes in enumerate((2, 1)):
+            for j in range(PACK):
+                gather = scalar_gather if j < scalar_planes else nc.vector.tensor_copy
+                gather(out=runs[h][:, j, :], in_=nodes(0, j, h * HALF, (h + 1) * HALF))
+        woven0 = [keep.tile([P, HALF, PACK], BF16, name="woven%d" % h, align_bytes=64) for h in range(2)]
         for h in range(2):
-            for j in range(2):
-                nc.scalar.activation(out=runs[h][:, j, :], in_=planes[j].indirect(halves[h]), func=COPY)
-                nc.vector.tensor_copy(out=runs[h][:, 2 + j, :], in_=planes[2 + j].indirect(halves[h]))
+            weave(nc.vector.tensor_copy, woven0[h], runs[h], slice(0, HALF))
         for h in range(2):
             cols = slice(h * HALF, (h + 1) * HALF)
-            woven = keep.tile([P, HALF, PACK], BF16, name="woven%d" % h, align_bytes=64)
-            nc.vector.tensor_copy(
-                out=woven[:].rearrange("p (c i) j -> p c j i", i=PACK),
-                in_=runs[h][:].rearrange("p j (c i) -> p c j i", i=PACK),
-            )
-            nc.vector.quantize_mx(out=x0_codes[:, cols].bitcast(FP8X4), scales=x0_scales[:, cols], in_=woven[:].rearrange("p c j -> p (c j)"))
+            quantize(x0_codes[:, cols], x0_scales[:, cols], woven0[h][:])
+
+        x_bf = keep.tile([P, S, PACK], BF16, name="x_bf", align_bytes=64)
         pair = keep.tile([P, 2, S], F32, name="pair")
-        nc.scalar.activation(out=pair[:, 0, :], in_=planes[PACK].indirect(picked[:]), func=COPY)
-        nc.vector.tensor_copy(out=pair[:, 1, :], in_=planes[PACK + 1].indirect(picked[:]))
-        nc.scalar.copy(out=x_bf[1][:, :, 0:2], in_=pair[:].rearrange("p j c -> p c j"))
-        gather(1, 2, 0, S)
-        middle = keep.tile([P, S - REST - STEPPED], BF16, name="middle")
-        nc.scalar.activation(out=middle[:], in_=planes[2 * PACK - 1].indirect(picked[:, STEPPED // LANES : (S - REST) // LANES]), func=COPY)
-        gather(1, PACK - 1, 0, STEPPED)
-        nc.vector.tensor_copy(out=x_bf[1][:, STEPPED : S - REST, PACK - 1], in_=middle[:])
+        scalar_gather(out=pair[:, 0, :], in_=nodes(1, 0, 0, S))
+        nc.vector.tensor_copy(out=pair[:, 1, :], in_=nodes(1, 1, 0, S))
+        for copy, cols in ((nc.vector.tensor_copy, slice(0, HALF)), (nc.scalar.copy, slice(HALF, S))):
+            copy(out=x_bf[:, cols, 0:2], in_=pair[:, :, cols].rearrange("p j c -> p c j"))
+        nc.vector.tensor_copy(out=x_bf[:, :, 2], in_=nodes(1, 2, 0, S))
+        run = keep.tile([P, HALF], BF16, name="run")
+        scalar_gather(out=run[:], in_=nodes(1, 3, 0, HALF))
+        nc.vector.tensor_copy(out=x_bf[:, HALF:S, 3], in_=nodes(1, 3, HALF, S))
+        nc.vector.tensor_copy(out=x_bf[:, 0:HALF, 3], in_=run[:])
 
-        pieces = ((0, HALF), (HALF, HALF + QUARTER), (HALF + QUARTER, S))
-        acc = [psum.tile([P, c1 - c0], F32, name="acc%d" % i) for i, (c0, c1) in enumerate(pieces)]
-        w0_codes, w0_scales = weave_w(0, ((nc.scalar.copy, slice(0, N)),))
-        for i, (c0, c1) in enumerate(pieces):
+        w_bf = [keep.tile([P, N, PACK], BF16, name="w_bf%d" % z, align_bytes=64) for z in range(PASSES)]
+        w_codes = [keep.tile([P, N], U32, name="w_codes%d" % z, align_bytes=64) for z in range(PASSES)]
+        w_scales = [keep.tile([P, N], U8, name="w_scales%d" % z, align_bytes=64) for z in range(PASSES)]
+        weave(nc.scalar.copy, w_bf[0], w_raw[0], slice(0, N))
+        quantize(w_codes[0][:], w_scales[0][:], w_bf[0][:])
+        weave(nc.scalar.copy, w_bf[1], w_raw[1], slice(0, W1_SCALAR))
+        weave(nc.vector.tensor_copy, w_bf[1], w_raw[1], slice(W1_SCALAR, N))
+
+        first_codes = tied.tile([P, PIECE], U32, name="first_codes", offset=0, align_bytes=64)
+        later_codes = tied.tile([P, S - PIECE], U32, name="later_codes", offset=RAW_BYTES, align_bytes=64)
+        x1_scales = keep.tile([P, S], U8, name="x1_scales", align_bytes=64)
+        pieces = [slice(i * PIECE, (i + 1) * PIECE) for i in range(PIECES)]
+        x1_codes = [first_codes[:]] + [later_codes[:, cols] for cols in pieces[:-1]]
+        for i, cols in enumerate(pieces):
+            quantize(x1_codes[i], x1_scales[:, cols], x_bf[:, cols, :])
+            if i == 0:
+                quantize(w_codes[1][:], w_scales[1][:], w_bf[1][:])
+
+        acc = [psum.tile([P, PIECE], F32, name="acc%d" % i) for i in range(PIECES)]
+
+        def product(i, z, codes, scales):
             nc.tensor.matmul_mx(
                 out=acc[i][:],
-                lhsT=w0_codes[:].bitcast(FP8X4),
-                lhsT_scale=w0_scales[:],
-                rhs=x0_codes[:, c0:c1].bitcast(FP8X4),
-                rhs_scale=x0_scales[:, c0:c1],
-                start=True,
-                stop=False,
+                lhsT=w_codes[z][:].bitcast(FP8X4),
+                lhsT_scale=w_scales[z][:],
+                rhs=codes.bitcast(FP8X4),
+                rhs_scale=scales,
+                start=z == 0,
+                stop=z == PASSES - 1,
             )
-        rest = tied.tile([P, REST], BF16, name="rest", offset=HALF * 4, align_bytes=64)
-        nc.vector.tensor_copy(out=rest[:], in_=planes[2 * PACK - 1].indirect(picked[:, (S - REST) // LANES : S // LANES]))
-        early_codes = tied.tile([P, HALF], U32, name="early_codes", offset=0, align_bytes=64)
-        early_scales = keep.tile([P, HALF], U8, name="early_scales", align_bytes=64)
-        nc.vector.quantize_mx(out=early_codes[:].bitcast(FP8X4), scales=early_scales[:], in_=x_bf[1][:, 0:HALF, :].rearrange("p c j -> p (c j)"))
-        x1 = [(early_codes[:], early_scales[:])]
-        w1_codes, w1_scales = weave_w(1, ((nc.scalar.copy, slice(0, W_SCALAR)), (nc.vector.tensor_copy, slice(W_SCALAR, N))))
-        nc.scalar.copy(out=x_bf[1][:, S - REST : S, PACK - 1], in_=rest[:])
-        late_codes = tied.tile([P, HALF], U32, name="late_codes", offset=RAW_BYTES, align_bytes=64)
-        late_scales = keep.tile([P, HALF], U8, name="late_scales", align_bytes=64)
-        for c0, c1 in pieces[1:]:
-            cols = slice(c0 - HALF, c1 - HALF)
-            nc.vector.quantize_mx(
-                out=late_codes[:, cols].bitcast(FP8X4),
-                scales=late_scales[:, cols],
-                in_=x_bf[1][:, c0:c1, :].rearrange("p c j -> p (c j)"),
-            )
-            x1.append((late_codes[:, cols], late_scales[:, cols]))
 
+        for i, cols in enumerate(pieces):
+            product(i, 0, x0_codes[:, cols], x0_scales[:, cols])
         y = keep.tile([P, S], F32, name="y")
-        for i, (c0, c1) in enumerate(pieces):
-            nc.tensor.matmul_mx(
-                out=acc[i][:],
-                lhsT=w1_codes[:].bitcast(FP8X4),
-                lhsT_scale=w1_scales[:],
-                rhs=x1[i][0].bitcast(FP8X4),
-                rhs_scale=x1[i][1],
-                start=False,
-                stop=True,
-            )
-            if i == 1:
-                nc.vector.tensor_copy(out=y[:, c0:c1], in_=acc[i][:])
-            else:
-                nc.scalar.copy(out=y[:, c0:c1], in_=acc[i][:])
+        for i, cols in enumerate(pieces):
+            product(i, 1, x1_codes[i], x1_scales[:, cols])
+            copy = nc.vector.tensor_copy if i % 2 else nc.scalar.copy
+            copy(out=y[:, cols], in_=acc[i][:])
 
         near = [keep.tile([P, V], F32, name="near%d" % d) for d in range(3)]
         first, second = slice(0, V_HALF), slice(V_HALF, V)
@@ -170,10 +147,10 @@ def tile_picked_median_none_e_kernel(tc, xT, w1, offs, pos1, pos2, pos3, out):
 
         for cols in (first, second):
             nc.vector.tensor_copy(out=near[0][:, cols], in_=neighbours(0, cols))
-            nc.scalar.activation(out=near[1][:, cols], in_=neighbours(1, cols), func=COPY)
+            scalar_gather(out=near[1][:, cols], in_=neighbours(1, cols))
         nc.vector.tensor_copy(out=near[2][:, fourth], in_=neighbours(2, fourth))
         for cols in (first, third):
-            nc.scalar.activation(out=near[2][:, cols], in_=neighbours(2, cols), func=COPY)
+            scalar_gather(out=near[2][:, cols], in_=neighbours(2, cols))
         hi = keep.tile([P, V], F32, name="hi")
         lo = keep.tile([P, V], F32, name="lo")
         capped = keep.tile([P, V], F32, name="capped")

@@ -76,7 +76,7 @@ def tile_picked_median_none_e_kernel(tc, xT, w1, offs, pos1, pos2, pos3, out):
         x0_codes = keep.tile([P, S], U32, name="x0_codes", align_bytes=64)
         x0_scales = keep.tile([P, S], U8, name="x0_scales", align_bytes=64)
         runs = [keep.tile([P, PACK, HALF], F32, name="runs%d" % h) for h in range(2)]
-        for h, scalar_planes in enumerate((2, 1)):
+        for h, scalar_planes in enumerate((1, 1)):
             for j in range(PACK):
                 gather = scalar_gather if j < scalar_planes else nc.vector.tensor_copy
                 gather(out=runs[h][:, j, :], in_=nodes(0, j, h * HALF, (h + 1) * HALF))
@@ -88,16 +88,20 @@ def tile_picked_median_none_e_kernel(tc, xT, w1, offs, pos1, pos2, pos3, out):
             quantize(x0_codes[:, cols], x0_scales[:, cols], woven0[h][:])
 
         x_bf = keep.tile([P, S, PACK], BF16, name="x_bf", align_bytes=64)
-        pair = keep.tile([P, 2, S], F32, name="pair")
-        scalar_gather(out=pair[:, 0, :], in_=nodes(1, 0, 0, S))
-        nc.vector.tensor_copy(out=pair[:, 1, :], in_=nodes(1, 1, 0, S))
-        for copy, cols in ((nc.vector.tensor_copy, slice(0, HALF)), (nc.scalar.copy, slice(HALF, S))):
-            copy(out=x_bf[:, cols, 0:2], in_=pair[:, :, cols].rearrange("p j c -> p c j"))
-        nc.vector.tensor_copy(out=x_bf[:, :, 2], in_=nodes(1, 2, 0, S))
+        low, high = slice(0, HALF), slice(HALF, S)
+        pair = keep.tile([P, 2, HALF], F32, name="pair")
+        triple = keep.tile([P, 3, HALF], F32, name="triple")
+        scalar_gather(out=pair[:, 0, :], in_=nodes(1, 0, HALF, S))
+        nc.vector.tensor_copy(out=pair[:, 1, :], in_=nodes(1, 1, HALF, S))
+        for j in range(3):
+            scalar_gather(out=triple[:, j, :], in_=nodes(1, j, 0, HALF))
+        nc.vector.tensor_copy(out=x_bf[:, high, 0:2], in_=pair[:].rearrange("p j c -> p c j"))
+        nc.vector.tensor_copy(out=x_bf[:, high, 2], in_=nodes(1, 2, HALF, S))
+        nc.vector.tensor_copy(out=x_bf[:, low, 0:3], in_=triple[:].rearrange("p j c -> p c j"))
         run = keep.tile([P, HALF], BF16, name="run")
         scalar_gather(out=run[:], in_=nodes(1, 3, 0, HALF))
-        nc.vector.tensor_copy(out=x_bf[:, HALF:S, 3], in_=nodes(1, 3, HALF, S))
-        nc.vector.tensor_copy(out=x_bf[:, 0:HALF, 3], in_=run[:])
+        nc.vector.tensor_copy(out=x_bf[:, high, 3], in_=nodes(1, 3, HALF, S))
+        nc.vector.tensor_copy(out=x_bf[:, low, 3], in_=run[:])
 
         w_bf = [keep.tile([P, N, PACK], BF16, name="w_bf%d" % z, align_bytes=64) for z in range(PASSES)]
         w_codes = [keep.tile([P, N], U32, name="w_codes%d" % z, align_bytes=64) for z in range(PASSES)]

@@ -26,7 +26,8 @@ PIECES = S // PIECE
 V_HALF = V // 2
 V_LAST = 64
 RAW_BYTES = PACK * N * 4
-W1_SCALAR = 64
+W1_SCALAR = 96
+RUN = 160
 
 
 def tile_picked_median_none_e_kernel(tc, xT, w1, offs, pos1, pos2, pos3, out):
@@ -98,10 +99,10 @@ def tile_picked_median_none_e_kernel(tc, xT, w1, offs, pos1, pos2, pos3, out):
         nc.vector.tensor_copy(out=x_bf[:, high, 0:2], in_=pair[:].rearrange("p j c -> p c j"))
         nc.vector.tensor_copy(out=x_bf[:, high, 2], in_=nodes(1, 2, HALF, S))
         nc.vector.tensor_copy(out=x_bf[:, low, 0:3], in_=triple[:].rearrange("p j c -> p c j"))
-        run = keep.tile([P, HALF], BF16, name="run")
-        scalar_gather(out=run[:], in_=nodes(1, 3, 0, HALF))
-        nc.vector.tensor_copy(out=x_bf[:, high, 3], in_=nodes(1, 3, HALF, S))
-        nc.vector.tensor_copy(out=x_bf[:, low, 3], in_=run[:])
+        run = keep.tile([P, RUN], BF16, name="run")
+        scalar_gather(out=run[:], in_=nodes(1, 3, 0, RUN))
+        nc.vector.tensor_copy(out=x_bf[:, RUN:S, 3], in_=nodes(1, 3, RUN, S))
+        nc.vector.tensor_copy(out=x_bf[:, 0:RUN, 3], in_=run[:])
 
         w_bf = [keep.tile([P, N, PACK], BF16, name="w_bf%d" % z, align_bytes=64) for z in range(PASSES)]
         w_codes = [keep.tile([P, N], U32, name="w_codes%d" % z, align_bytes=64) for z in range(PASSES)]

@@ -22,7 +22,6 @@ PASSES = K // K_PASS
 LANES = 16
 HALF = S // 2
 PIECE = 128
-PIECES = S // PIECE
 V_HALF = V // 2
 V_LAST = 64
 RAW_BYTES = PACK * N * 4
@@ -76,17 +75,13 @@ def tile_picked_median_none_e_kernel(tc, xT, w1, offs, pos1, pos2, pos3, out):
 
         x0_codes = keep.tile([P, S], U32, name="x0_codes", align_bytes=64)
         x0_scales = keep.tile([P, S], U8, name="x0_scales", align_bytes=64)
-        runs = [keep.tile([P, PACK, HALF], F32, name="runs%d" % h) for h in range(2)]
-        for h, scalar_planes in enumerate((1, 1)):
-            for j in range(PACK):
-                gather = scalar_gather if j < scalar_planes else nc.vector.tensor_copy
-                gather(out=runs[h][:, j, :], in_=nodes(0, j, h * HALF, (h + 1) * HALF))
-        woven0 = [keep.tile([P, HALF, PACK], BF16, name="woven%d" % h, align_bytes=64) for h in range(2)]
-        for h in range(2):
-            weave(nc.vector.tensor_copy, woven0[h], runs[h], slice(0, HALF))
-        for h in range(2):
-            cols = slice(h * HALF, (h + 1) * HALF)
-            quantize(x0_codes[:, cols], x0_scales[:, cols], woven0[h][:])
+        runs = keep.tile([P, PACK, S], F32, name="runs")
+        for j in range(PACK):
+            gather = scalar_gather if j == 0 else nc.vector.tensor_copy
+            gather(out=runs[:, j, :], in_=nodes(0, j, 0, S))
+        woven = keep.tile([P, S, PACK], BF16, name="woven", align_bytes=64)
+        weave(nc.vector.tensor_copy, woven, runs, slice(0, S))
+        quantize(x0_codes[:], x0_scales[:], woven[:])
 
         x_bf = keep.tile([P, S, PACK], BF16, name="x_bf", align_bytes=64)
         low, high = slice(0, HALF), slice(HALF, S)
@@ -115,14 +110,14 @@ def tile_picked_median_none_e_kernel(tc, xT, w1, offs, pos1, pos2, pos3, out):
         first_codes = tied.tile([P, PIECE], U32, name="first_codes", offset=0, align_bytes=64)
         later_codes = tied.tile([P, S - PIECE], U32, name="later_codes", offset=RAW_BYTES, align_bytes=64)
         x1_scales = keep.tile([P, S], U8, name="x1_scales", align_bytes=64)
-        pieces = [slice(i * PIECE, (i + 1) * PIECE) for i in range(PIECES)]
-        x1_codes = [first_codes[:]] + [later_codes[:, cols] for cols in pieces[:-1]]
+        pieces = (slice(0, PIECE), slice(PIECE, S - PIECE), slice(S - PIECE, S))
+        x1_codes = [first_codes[:]] + [later_codes[:, cols.start - PIECE : cols.stop - PIECE] for cols in pieces[1:]]
         for i, cols in enumerate(pieces):
             quantize(x1_codes[i], x1_scales[:, cols], x_bf[:, cols, :])
             if i == 0:
                 quantize(w_codes[1][:], w_scales[1][:], w_bf[1][:])
 
-        acc = [psum.tile([P, PIECE], F32, name="acc%d" % i) for i in range(PIECES)]
+        acc = [psum.tile([P, cols.stop - cols.start], F32, name="acc%d" % i) for i, cols in enumerate(pieces)]
 
         def product(i, z, codes, scales):
             nc.tensor.matmul_mx(

@@ -27,6 +27,7 @@ V_LAST = 64
 RAW_BYTES = PACK * N * 4
 W1_SCALAR = 96
 RUN = 160
+PAIR_VECTOR = 128
 
 
 def tile_picked_median_none_e_kernel(tc, xT, w1, offs, pos1, pos2, pos3, out):
@@ -35,6 +36,11 @@ def tile_picked_median_none_e_kernel(tc, xT, w1, offs, pos1, pos2, pos3, out):
         keep = ctx.enter_context(tc.tile_pool(name="keep", bufs=1))
         tied = ctx.enter_context(tc.tile_pool(name="tied", bufs=1))
         psum = ctx.enter_context(tc.psum_pool(name="psum", bufs=1))
+
+        warm_in = keep.tile([P, 1], F32, name="warm_in")
+        warm_out = keep.tile([P, 1], F32, name="warm_out")
+        nc.gpsimd.memset(warm_in[:], 0.0)
+        nc.scalar.activation(out=warm_out[:], in_=warm_in[:], func=COPY)
 
         picked = keep.tile([P, S // LANES], U16, name="picked")
         x_pass = xT.rearrange("(z p j) t -> z p j t", p=P, j=PACK)
@@ -76,24 +82,24 @@ def tile_picked_median_none_e_kernel(tc, xT, w1, offs, pos1, pos2, pos3, out):
         x0_codes = keep.tile([P, S], U32, name="x0_codes", align_bytes=64)
         x0_scales = keep.tile([P, S], U8, name="x0_scales", align_bytes=64)
         runs = keep.tile([P, PACK, S], F32, name="runs")
-        for j in range(PACK):
-            gather = scalar_gather if j == 0 else nc.vector.tensor_copy
-            gather(out=runs[:, j, :], in_=nodes(0, j, 0, S))
         woven = keep.tile([P, S, PACK], BF16, name="woven", align_bytes=64)
-        weave(nc.vector.tensor_copy, woven, runs, slice(0, S))
-        quantize(x0_codes[:], x0_scales[:], woven[:])
+        halves = (slice(0, HALF), slice(HALF, S))
+        for j in (2, 3):
+            nc.vector.tensor_copy(out=runs[:, j, :], in_=nodes(0, j, 0, S))
+        for cols in halves:
+            for j in (0, 1):
+                scalar_gather(out=runs[:, j, cols], in_=nodes(0, j, cols.start, cols.stop))
+        for cols in halves:
+            weave(nc.vector.tensor_copy, woven, runs, cols)
+            quantize(x0_codes[:, cols], x0_scales[:, cols], woven[:, cols, :])
 
         x_bf = keep.tile([P, S, PACK], BF16, name="x_bf", align_bytes=64)
-        low, high = slice(0, HALF), slice(HALF, S)
-        pair = keep.tile([P, 2, HALF], F32, name="pair")
-        triple = keep.tile([P, 3, HALF], F32, name="triple")
-        scalar_gather(out=pair[:, 0, :], in_=nodes(1, 0, HALF, S))
-        nc.vector.tensor_copy(out=pair[:, 1, :], in_=nodes(1, 1, HALF, S))
-        for j in range(3):
-            scalar_gather(out=triple[:, j, :], in_=nodes(1, j, 0, HALF))
-        nc.vector.tensor_copy(out=x_bf[:, high, 0:2], in_=pair[:].rearrange("p j c -> p c j"))
-        nc.vector.tensor_copy(out=x_bf[:, high, 2], in_=nodes(1, 2, HALF, S))
-        nc.vector.tensor_copy(out=x_bf[:, low, 0:3], in_=triple[:].rearrange("p j c -> p c j"))
+        pair = keep.tile([P, 2, S], F32, name="pair")
+        scalar_gather(out=pair[:, 0, :], in_=nodes(1, 0, 0, S))
+        nc.vector.tensor_copy(out=pair[:, 1, :], in_=nodes(1, 1, 0, S))
+        for copy, cols in ((nc.vector.tensor_copy, slice(0, PAIR_VECTOR)), (nc.scalar.copy, slice(PAIR_VECTOR, S))):
+            copy(out=x_bf[:, cols, 0:2], in_=pair[:, :, cols].rearrange("p j c -> p c j"))
+        nc.vector.tensor_copy(out=x_bf[:, :, 2], in_=nodes(1, 2, 0, S))
         run = keep.tile([P, RUN], BF16, name="run")
         scalar_gather(out=run[:], in_=nodes(1, 3, 0, RUN))
         nc.vector.tensor_copy(out=x_bf[:, RUN:S, 3], in_=nodes(1, 3, RUN, S))
@@ -107,11 +113,11 @@ def tile_picked_median_none_e_kernel(tc, xT, w1, offs, pos1, pos2, pos3, out):
         weave(nc.scalar.copy, w_bf[1], w_raw[1], slice(0, W1_SCALAR))
         weave(nc.vector.tensor_copy, w_bf[1], w_raw[1], slice(W1_SCALAR, N))
 
-        first_codes = tied.tile([P, PIECE], U32, name="first_codes", offset=0, align_bytes=64)
-        later_codes = tied.tile([P, S - PIECE], U32, name="later_codes", offset=RAW_BYTES, align_bytes=64)
+        first_codes = tied.tile([P, HALF], U32, name="first_codes", offset=0, align_bytes=64)
+        later_codes = tied.tile([P, HALF], U32, name="later_codes", offset=RAW_BYTES, align_bytes=64)
         x1_scales = keep.tile([P, S], U8, name="x1_scales", align_bytes=64)
-        pieces = (slice(0, PIECE), slice(PIECE, S - PIECE), slice(S - PIECE, S))
-        x1_codes = [first_codes[:]] + [later_codes[:, cols.start - PIECE : cols.stop - PIECE] for cols in pieces[1:]]
+        pieces = (slice(0, HALF), slice(HALF, S - PIECE), slice(S - PIECE, S))
+        x1_codes = [first_codes[:]] + [later_codes[:, cols.start - HALF : cols.stop - HALF] for cols in pieces[1:]]
         for i, cols in enumerate(pieces):
             quantize(x1_codes[i], x1_scales[:, cols], x_bf[:, cols, :])
             if i == 0:

@@ -146,7 +146,7 @@ def tile_picked_median_none_e_kernel(tc, xT, w1, offs, pos1, pos2, pos3, out):
 
         near = [keep.tile([P, V], F32, name="near%d" % d) for d in range(3)]
         first, second = slice(0, V_HALF), slice(V_HALF, V)
-        third, fourth = slice(V_HALF, V - V_LAST), slice(V - V_LAST, V)
+        quarters = [slice(c, c + V_LAST) for c in range(0, V, V_LAST)]
 
         def neighbours(d, cols):
             return y[:].indirect(places[d][:, cols.start // LANES : cols.stop // LANES])
@@ -154,19 +154,26 @@ def tile_picked_median_none_e_kernel(tc, xT, w1, offs, pos1, pos2, pos3, out):
         for cols in (first, second):
             nc.vector.tensor_copy(out=near[0][:, cols], in_=neighbours(0, cols))
             scalar_gather(out=near[1][:, cols], in_=neighbours(1, cols))
-        nc.vector.tensor_copy(out=near[2][:, fourth], in_=neighbours(2, fourth))
-        for cols in (first, third):
+        nc.vector.tensor_copy(out=near[2][:, quarters[0]], in_=neighbours(2, quarters[0]))
+        for cols in quarters[1:]:
             scalar_gather(out=near[2][:, cols], in_=neighbours(2, cols))
         hi = keep.tile([P, V], F32, name="hi")
         lo = keep.tile([P, V], F32, name="lo")
         capped = keep.tile([P, V], F32, name="capped")
         med = keep.tile([P, V], F32, name="med")
-        for cols in (first, second):
-            nc.vector.tensor_tensor(out=hi[:, cols], in0=near[0][:, cols], in1=near[1][:, cols], op=MAX)
-            nc.vector.tensor_tensor(out=lo[:, cols], in0=near[0][:, cols], in1=near[1][:, cols], op=MIN)
-        for cols in (fourth, first, third):
-            nc.vector.tensor_tensor(out=capped[:, cols], in0=hi[:, cols], in1=near[2][:, cols], op=MIN)
-        for cols in (first, fourth, third):
-            nc.vector.tensor_tensor(out=med[:, cols], in0=lo[:, cols], in1=capped[:, cols], op=MAX)
+        steps = (
+            (hi, near[0], near[1], MAX, first),
+            (lo, near[0], near[1], MIN, first),
+            (hi, near[0], near[1], MAX, second),
+            (capped, hi, near[2], MIN, first),
+            (lo, near[0], near[1], MIN, second),
+            (capped, hi, near[2], MIN, quarters[2]),
+            (capped, hi, near[2], MIN, quarters[3]),
+            (med, lo, capped, MAX, first),
+            (med, lo, capped, MAX, quarters[2]),
+            (med, lo, capped, MAX, quarters[3]),
+        )
+        for result, in0, in1, op, cols in steps:
+            nc.vector.tensor_tensor(out=result[:, cols], in0=in0[:, cols], in1=in1[:, cols], op=op)
         for cols in (first, second):
             nc.sync.dma_start(out=out[:, cols], in_=med[:, cols])

@@ -63,6 +63,9 @@ def tile_picked_median_none_e_kernel(tc, xT, w1, offs, pos1, pos2, pos3, out):
             place = keep.tile([P, V // LANES], U16, name="place%d" % d)
             nc.sync.dma_start(out=place[:], in_=pos)
             places.append(place)
+        for e in range(4):
+            extra = keep.tile([P, 16], F32, name="extra%d" % e)
+            nc.sync.dma_start(out=extra[:], in_=w_pass[0, :, e, 0:16])
 
         def nodes(z, j, lo, hi):
             return planes[z, j].indirect(picked[:, lo // LANES : hi // LANES])

from contextlib import ExitStack

import concourse.mybir as mybir

K, T, S, V, N = 1024, 2048, 512, 256, 128
FLOPS = 2 * K * S * N

F32 = mybir.dt.float32
BF16 = mybir.dt.bfloat16
U32 = mybir.dt.uint32
U16 = mybir.dt.uint16
U8 = mybir.dt.uint8
FP8X4 = mybir.dt.float8_e4m3fn_x4
MAX = mybir.AluOpType.max
MIN = mybir.AluOpType.min
COPY = mybir.ActivationFunctionType.Copy

P = 128
PACK = 4
K_PASS = P * PACK
PASSES = K // K_PASS
LANES = 16
HALF = S // 2
PIECE = 128
V_HALF = V // 2
V_LAST = 64
RAW_BYTES = PACK * N * 4
W1_SCALAR = 96
RUN = 160
PAIR_VECTOR = 128


def tile_picked_median_none_e_kernel(tc, xT, w1, offs, pos1, pos2, pos3, out):
    nc = tc.nc
    with ExitStack() as ctx:
        keep = ctx.enter_context(tc.tile_pool(name="keep", bufs=1))
        tied = ctx.enter_context(tc.tile_pool(name="tied", bufs=1))
        psum = ctx.enter_context(tc.psum_pool(name="psum", bufs=1))

        warm_in = keep.tile([P, 1], F32, name="warm_in")
        warm_out = keep.tile([P, 1], F32, name="warm_out")
        nc.gpsimd.memset(warm_in[:], 0.0)
        nc.scalar.activation(out=warm_out[:], in_=warm_in[:], func=COPY)

        picked = keep.tile([P, S // LANES], U16, name="picked")
        x_pass = xT.rearrange("(z p j) t -> z p j t", p=P, j=PACK)
        w_pass = w1.rearrange("(z p j) n -> z p j n", p=P, j=PACK)
        planes = {}
        for i, (z, j0, j1) in enumerate(((0, 0, 4), (1, 0, 2), (1, 2, 3), (1, 3, 4))):
            rows = keep.tile([P, j1 - j0, T], F32, name="rows%d" % i)
            nc.sync.dma_start(out=rows[:], in_=x_pass[z, :, j0:j1, :])
            if i == 0:
                nc.sync.dma_start(out=picked[:], in_=offs)
            for j in range(j0, j1):
                planes[z, j] = rows[:, j - j0, :]
        w_raw = []
        for z in range(PASSES):
            raw = tied.tile([P, PACK, N], F32, name="w_raw%d" % z, offset=z * RAW_BYTES, align_bytes=64)
            nc.sync.dma_start(out=raw[:], in_=w_pass[z])
            w_raw.append(raw)
        places = []
        for d, pos in enumerate((pos1, pos2, pos3)):
            place = keep.tile([P, V // LANES], U16, name="place%d" % d)
            nc.sync.dma_start(out=place[:], in_=pos)
            places.append(place)
        for e in range(4):
            extra = keep.tile([P, 16], F32, name="extra%d" % e)
            nc.sync.dma_start(out=extra[:], in_=w_pass[0, :, e, 0:16])

        def nodes(z, j, lo, hi):
            return planes[z, j].indirect(picked[:, lo // LANES : hi // LANES])

        def scalar_gather(out, in_):
            nc.scalar.activation(out=out, in_=in_, func=COPY)

        def weave(copy, woven, raw, cols):
            copy(
                out=woven[:, cols, :].rearrange("p (c i) j -> p c j i", i=PACK),
                in_=raw[:, :, cols].rearrange("p j (c i) -> p c j i", i=PACK),
            )

        def quantize(codes, scales, woven):
            nc.vector.quantize_mx(out=codes.bitcast(FP8X4), scales=scales, in_=woven.rearrange("p c j -> p (c j)"))

        x0_codes = keep.tile([P, S], U32, name="x0_codes", align_bytes=64)
        x0_scales = keep.tile([P, S], U8, name="x0_scales", align_bytes=64)
        runs = keep.tile([P, PACK, S], F32, name="runs")
        woven = keep.tile([P, S, PACK], BF16, name="woven", align_bytes=64)
        halves = (slice(0, HALF), slice(HALF, S))
        for j in (2, 3):
            nc.vector.tensor_copy(out=runs[:, j, :], in_=nodes(0, j, 0, S))
        for cols in halves:
            for j in (0, 1):
                scalar_gather(out=runs[:, j, cols], in_=nodes(0, j, cols.start, cols.stop))
        for cols in halves:
            weave(nc.vector.tensor_copy, woven, runs, cols)
            quantize(x0_codes[:, cols], x0_scales[:, cols], woven[:, cols, :])

        x_bf = keep.tile([P, S, PACK], BF16, name="x_bf", align_bytes=64)
        pair = keep.tile([P, 2, S], F32, name="pair")
        scalar_gather(out=pair[:, 0, :], in_=nodes(1, 0, 0, S))
        nc.vector.tensor_copy(out=pair[:, 1, :], in_=nodes(1, 1, 0, S))
        for copy, cols in ((nc.vector.tensor_copy, slice(0, PAIR_VECTOR)), (nc.scalar.copy, slice(PAIR_VECTOR, S))):
            copy(out=x_bf[:, cols, 0:2], in_=pair[:, :, cols].rearrange("p j c -> p c j"))
        nc.vector.tensor_copy(out=x_bf[:, :, 2], in_=nodes(1, 2, 0, S))
        run = keep.tile([P, RUN], BF16, name="run")
        scalar_gather(out=run[:], in_=nodes(1, 3, 0, RUN))
        nc.vector.tensor_copy(out=x_bf[:, RUN:S, 3], in_=nodes(1, 3, RUN, S))
        nc.vector.tensor_copy(out=x_bf[:, 0:RUN, 3], in_=run[:])

        w_bf = [keep.tile([P, N, PACK], BF16, name="w_bf%d" % z, align_bytes=64) for z in range(PASSES)]
        w_codes = [keep.tile([P, N], U32, name="w_codes%d" % z, align_bytes=64) for z in range(PASSES)]
        w_scales = [keep.tile([P, N], U8, name="w_scales%d" % z, align_bytes=64) for z in range(PASSES)]
        weave(nc.scalar.copy, w_bf[0], w_raw[0], slice(0, N))
        quantize(w_codes[0][:], w_scales[0][:], w_bf[0][:])
        weave(nc.scalar.copy, w_bf[1], w_raw[1], slice(0, W1_SCALAR))
        weave(nc.vector.tensor_copy, w_bf[1], w_raw[1], slice(W1_SCALAR, N))

        first_codes = tied.tile([P, HALF], U32, name="first_codes", offset=0, align_bytes=64)
        later_codes = tied.tile([P, HALF], U32, name="later_codes", offset=RAW_BYTES, align_bytes=64)
        x1_scales = keep.tile([P, S], U8, name="x1_scales", align_bytes=64)
        pieces = (slice(0, HALF), slice(HALF, S - PIECE), slice(S - PIECE, S))
        x1_codes = [first_codes[:]] + [later_codes[:, cols.start - HALF : cols.stop - HALF] for cols in pieces[1:]]
        for i, cols in enumerate(pieces):
            quantize(x1_codes[i], x1_scales[:, cols], x_bf[:, cols, :])
            if i == 0:
                quantize(w_codes[1][:], w_scales[1][:], w_bf[1][:])

        acc = [psum.tile([P, cols.stop - cols.start], F32, name="acc%d" % i) for i, cols in enumerate(pieces)]

        def product(i, z, codes, scales):
            nc.tensor.matmul_mx(
                out=acc[i][:],
                lhsT=w_codes[z][:].bitcast(FP8X4),
                lhsT_scale=w_scales[z][:],
                rhs=codes.bitcast(FP8X4),
                rhs_scale=scales,
                start=z == 0,
                stop=z == PASSES - 1,
            )

        for i, cols in enumerate(pieces):
            product(i, 0, x0_codes[:, cols], x0_scales[:, cols])
        y = keep.tile([P, S], F32, name="y")
        for i, cols in enumerate(pieces):
            product(i, 1, x1_codes[i], x1_scales[:, cols])
            copy = nc.vector.tensor_copy if i % 2 else nc.scalar.copy
            copy(out=y[:, cols], in_=acc[i][:])

        near = [keep.tile([P, V], F32, name="near%d" % d) for d in range(3)]
        first, second = slice(0, V_HALF), slice(V_HALF, V)
        quarters = [slice(c, c + V_LAST) for c in range(0, V, V_LAST)]

        def neighbours(d, cols):
            return y[:].indirect(places[d][:, cols.start // LANES : cols.stop // LANES])

        for cols in (first, second):
            nc.vector.tensor_copy(out=near[0][:, cols], in_=neighbours(0, cols))
            scalar_gather(out=near[1][:, cols], in_=neighbours(1, cols))
        nc.vector.tensor_copy(out=near[2][:, quarters[0]], in_=neighbours(2, quarters[0]))
        for cols in quarters[1:]:
            scalar_gather(out=near[2][:, cols], in_=neighbours(2, cols))
        hi = keep.tile([P, V], F32, name="hi")
        lo = keep.tile([P, V], F32, name="lo")
        capped = keep.tile([P, V], F32, name="capped")
        med = keep.tile([P, V], F32, name="med")
        steps = (
            (hi, near[0], near[1], MAX, first),
            (lo, near[0], near[1], MIN, first),
            (hi, near[0], near[1], MAX, second),
            (capped, hi, near[2], MIN, first),
            (lo, near[0], near[1], MIN, second),
            (capped, hi, near[2], MIN, quarters[2]),
            (capped, hi, near[2], MIN, quarters[3]),
            (med, lo, capped, MAX, first),
            (med, lo, capped, MAX, quarters[2]),
            (med, lo, capped, MAX, quarters[3]),
        )
        for result, in0, in1, op, cols in steps:
            nc.vector.tensor_tensor(out=result[:, cols], in0=in0[:, cols], in1=in1[:, cols], op=op)
        for cols in (first, second):
            nc.sync.dma_start(out=out[:, cols], in_=med[:, cols])
